import numpy as np, ml_dtypes
CORES = [36,164,52,180,100,228,116,244]
N = 8
import mx_ref
BF = ml_dtypes.bfloat16
def gentries(a):
    return np.ascontiguousarray(a.reshape(8, 16, -1).transpose(0, 2, 1)).reshape(8, -1)
def gtable(e):
    e = np.asarray(e); return np.ascontiguousarray(e.reshape(8, -1, 16).transpose(0, 2, 1)).reshape(128, -1).astype(np.int32)
def gcols(t, e):
    v = np.concatenate([t.reshape(8, 16, -1, 4), np.zeros((8, 16, 1, 4), BF)], axis=2)
    return np.ascontiguousarray(np.stack([v[g][:, e[g]] for g in range(8)])).reshape(128, -1)
def tile(rs):
    return np.stack(rs, axis=2).reshape(128, -1).astype(BF)
def pick(q, e):
    c = np.concatenate([q[0].reshape(128, -1, 4), np.zeros((128, 1, 4), np.uint8)], axis=1); s = np.concatenate([q[1], np.ones((16, 1), np.uint8)], axis=1)
    return (np.ascontiguousarray(c[:, e].reshape(128, -1)), np.ascontiguousarray(s[:, e]))
def join(*qs):
    return (np.concatenate([q[0] for q in qs], axis=1), np.concatenate([q[1] for q in qs], axis=1))
def put(q, e, v):
    c, s = q[0].reshape(128, -1, 4).copy(), q[1].copy(); c[:, e] = v[0].reshape(128, -1, 4); s[:, e] = v[1]
    return (c.reshape(128, -1), s)
def pk(c, s):
    return (np.ascontiguousarray(c), mx_ref.live(s))
def emit(q):
    return q[0], q[1]
def packed(v, rng):
    q = [mx_ref.quantize(np.ascontiguousarray(v[r])) for r in range(N)]
    return np.stack([a for a, b in q]), np.stack([mx_ref.plane(b, rng) for a, b in q])
def values_of_codes():
    e, c = np.zeros((128, 128, 4), np.float32), np.zeros((128, 2, 4), np.uint8)
    e[np.arange(128), np.arange(128), 0] = 1
    c[:127, :, 0] = np.arange(256).reshape(2, 128).T[:127]
    return mx_ref.matmul(mx_ref.quantize(e.reshape(128, 512).astype(BF)), (c.reshape(128, 8), np.full((16, 2), 127, np.uint8))).T.reshape(-1).astype(np.float64)
CODE_VALUE, SCALE_VALUE = values_of_codes(), 2.0 ** (np.arange(256) - 127.0)
def decode(q):
    return (CODE_VALUE[q[0]].reshape(16, 8, -1, 4) * SCALE_VALUE[q[1]][:, None, :, None] + 0.0).reshape(128, -1).astype(np.float32)
def f(rng, *shape):
    return mx_ref.flush((rng.standard_normal(shape, dtype=np.float32) * np.exp2(rng.integers(-2, 3, shape[:-1] + (1,)))).astype(BF))
def wide(rng, *shape, cols=0):
    v = rng.standard_normal(shape, dtype=np.float32) * np.exp2(rng.integers(-12, 13, shape)).astype(np.float32)
    if cols: v *= np.repeat(np.exp2(rng.integers(-cols, cols + 1, shape[:-2] + (1, shape[-1] // 4))) * (rng.random(shape[:-2] + (1, shape[-1] // 4)) > 0.0625), 4, axis=-1).astype(np.float32)
    return mx_ref.flush(v.astype(BF))
C = 320
MASK = [4, 1, 2]
def numbers_of(rng):
    return {"x": np.array(f(rng, N, 128, 4 * C)), "u": np.array(f(rng, N, 128, 512)), "v": np.array(f(rng, N, 128, 512))}
def following(o):
    e = np.zeros_like(o)
    np.put_along_axis(e, o, np.roll(o, -1, axis=-1), axis=-1)
    return e
def rings(rng):
    return following(rng.permuted(np.tile(np.arange(C), (N, 8, 1)), axis=2))
def runs(rng, when, same=False):
    o, go = np.zeros((N, 8, C), np.int64), np.zeros((N, 8, C), bool)
    for r in range(N):
        k = rng.permutation(C)
        for g in range(8):
            p = r ^ MASK[when[g]]
            if p < r: continue
            if not same: k = rng.permutation(C)
            for i, m in ((r, [1, 0, 3, 2]), (p, [2, 0, 3, 1])):
                q = rng.permuted(k.reshape(4, -1), axis=1)[m]
                o[i, g] = np.concatenate([q[:2].T.reshape(-1), q[2:].T.reshape(-1)])
                go[i, g, q[:2].reshape(-1)] = True
    return following(o), go
def stored(e):
    return {"nx": np.stack([gtable(e[r]) for r in range(N)])}
def layers(rng, still=[]):
    w = np.array(f(rng, N, 128, 2048)).reshape(N, 8, 16, 4, 8, 16, 4)
    for i in still:
        w[:, :, i] = 0
        w[:, :, :, :, :, i] = 0
    return w
def weights(rng, w):
    c, s = packed(np.ascontiguousarray(w).reshape(N, 128, 2048), rng)
    return {"wc": c, "ws": s}
def setup_inputs(rng):
    return {**numbers_of(rng), **stored(rings(rng)), **weights(rng, layers(rng))}
def setup_inputs_ties(rng):
    d = numbers_of(rng)
    o = rng.permutation(N)
    k = rng.integers(-1, 2, (N, 8, C)).astype(np.float32)
    k[o[1]] = 1
    x = d["x"].reshape(N, 8, 16, C, 4)
    x[:, :, 0] = 0
    x[:, :, 0, :, 0] = k.astype(BF)
    c = np.ones(N, np.float32)
    c[o[0]] = 0
    c[o[2]] = -1
    u = d["u"].reshape(N, 128, 128, 4)
    u[:, :, ::16] = 0
    for h in range(0, 128, 16): u[:, h, h, 0] = c.astype(BF)
    e, i = rings(rng), np.arange(C)
    for r in range(N):
        p, h = r ^ MASK[0], rng.permutation(8)
        if p < r: continue
        e[p, h[0]] = e[r, h[0]]
        e[p, h[1]] = np.argsort(e[r, h[1]])
        e[r, h[2]], e[p, h[2]] = (i + 1) % C, (i - 1) % C
        e[r, h[3]] = e[p, h[3]] = (i + 1) % C
    w = layers(rng)
    w[:, :, :, :, :, :8] = 0
    return {"x": x.reshape(N, 128, 4 * C), "u": u.reshape(N, 128, 512), "v": d["v"], **stored(e), **weights(rng, w)}
def setup_inputs_near(rng):
    d = numbers_of(rng)
    o = rng.permutation(N) % 4
    k = np.where(o % 2 == 0, 1.0, 2.0 ** -30)
    x = np.zeros((N, 8, 16, C, 4))
    s = rng.integers(-1, 2, (N, 8, C)) * k[:, None, None]
    x[:, :, 0, :, 0] = 1.125 * s
    x[:, :, 1, :, 0] = -1.25 * s
    x[:, :, 8, :, 0] = rng.integers(-1, 2, (N, 8, C)) * 2.0 ** -27
    x[:, :, 8, :, 1] = 2.0 ** -27
    x[:, :, 9:] = (1.0 + rng.integers(0, 128, (N, 8, 7, C, 4)) * 2.0 ** -7) * 2.0 ** -27 * rng.choice([-1.0, 1.0], (N, 8, 7, C, 4))
    w = layers(rng, list(range(9)))
    for r in range(N):
        if o[r] % 2 == 1: x[r, :, 7, :, 0] = 2.0 ** -26
        if o[r] == 3:
            x[r, :, :2] = 0
            x[r, :, 7, :, 0] = 2.0 ** -27
            for g in range(8):
                w[r, g, 8, 0, g, 0, 0] = 2.0 ** -10
                w[r, g, 8, 0, g, 0, 1] = 2.0 ** -8
                w[r, g, 8, 0, g, 1, 0] = -2.0 ** -10
                w[r, g, 8, 0, g, 1, 1] = -1.125 * 2.0 ** -8
        else:
            at = [0, C - 1, int(rng.integers(C)), int(rng.integers(C))]
            for g, j in zip(rng.permutation(8)[:4], at): x[r, g, 0, j, 0] = 2.0 ** 30 * rng.choice([-1.0, 1.0])
    u = d["u"].reshape(N, 128, 128, 4)
    u[:, :, ::16] = 0
    for h in range(0, 128, 16):
        u[:, h, h, 0] = (1.125 * k).astype(np.float32).astype(BF)
        u[:, h + 1, h, 0] = k.astype(np.float32).astype(BF)
    return {"x": x.astype(np.float32).reshape(N, 128, 4 * C).astype(BF), "u": u.reshape(N, 128, 512), "v": d["v"], **stored(rings(rng)), **weights(rng, w)}
def setup_inputs_runs(rng):
    d = numbers_of(rng)
    o = rng.permutation(8)
    when = np.zeros(8, np.int64)
    when[o[4:6]] = 1
    when[o[6:]] = 2
    e, go = runs(rng, when)
    low = -rng.integers(0, 2, (N, 8, C))
    t = np.where(go, 1, low)
    for r in range(N):
        h = rng.permutation(o[:4])
        t[r, h[0]] = 1
        t[r, h[1]] = low[r, h[1]]
    for g in o[4:]:
        for i in range(when[g]): t[:, g] = np.take_along_axis(t[:, g], e[:, g], axis=1)
    x = (1.0 + (2 * rng.integers(0, 64, (N, 16, 8, C, 4)) + 1) * 2.0 ** -7) * np.exp2(-rng.integers(0, 7, (N, 16, 8, C, 4)).astype(np.float64)) * rng.choice([-1.0, 1.0], (N, 16, 8, C, 4))
    c = rng.choice([-1.0, 1.0], (N, 16, 1))
    k = np.exp2(when - 8.0)[:, None]
    x[:, :, 0, :, 0] = np.where(rng.random((N, 16, C)) < 0.5, 1.96875, 1.875) * 2.0 ** 8 * c
    x[:, :, 3, :, 0] = 1.875 * 2.0 ** 7
    x[:, ::2, 1, :, 0] = (8 + t) * k
    x[:, ::2, 2, :, 0] = 8 * k
    u = d["u"].reshape(N, 128, 128, 4)
    u[:, :, ::16] = 0
    for h in range(0, 128, 16):
        u[:, h + 1, h, 0] = 1
        u[:, h + 2, h, 0] = -1
    w = layers(rng, [0, 3, 8, 11])
    for g in range(8):
        for i in (0, 1):
            w[:, g, 8 * i + 3, 0, g, 8 * i, 0] = (64 * c[:, 2 * g + i, 0]).astype(np.float32).astype(BF)
            w[:, g, 8 * i + 3, 0, g, 8 * i + 3, 0] = 32
    for g in o[4:]:
        x[:, 2 * g, 4, :, 0] = -1.0
        x[:, 2 * g, 5, :, 0] = 1.0 - when[g]
        u[:, 16 * g + 4, 16 * g, 0] = 1
        for i in (1, 2, 4, 5): w[:, :, :, :, g, i] = 0
        w[:, g, 4, 0, g, 4, 0] = -32
        w[:, g, 5, 0, g, 4, 0] = 64
        w[:, g, 5, 0, g, 5, 0] = -32
    return {"x": x.astype(np.float32).reshape(N, 128, 4 * C).astype(BF), "u": u.reshape(N, 128, 512), "v": d["v"], **stored(e), **weights(rng, w)}
def setup_inputs_ends(rng):
    d = numbers_of(rng)
    e, go = runs(rng, np.zeros(8, np.int64), True)
    o = rng.permutation(N) % 4
    s = go[:, 0] * 2.0 - 1.0
    small = (1.0 + 0.125 * rng.integers(0, 8, (N, 8, 16, C, 4))) * 2.0 ** -20
    x = (0.9 + 0.1 * rng.random((N, 8, 16, C, 4))) * 2.0 ** 30
    u = d["u"].astype(np.float32).reshape(N, 128, 128, 4)
    v = np.zeros((N, 128, 512), np.float32)
    w = np.zeros((N, 128, 4, 128, 4), np.float32)
    i = np.arange(128)
    for r in range(N):
        if o[r] == 0: x[r] *= s[r][:, None]
        if o[r] == 1: x[r] *= -1
        if o[r] == 2: x[r] *= rng.choice([-1.0, 1.0], (8, 1, C, 1))
        if o[r] == 3: x[r] = small[r] * s[r][:, None]
        x[r, 7, 8:] = small[r, 7, 8:] * rng.choice([-1.0, 1.0], (8, C, 4))
        c = np.array([0.0, 1, 1, 1, -1, -1, -1, -1])[rng.permutation(8)][None, :, None]
        if o[r] < 3: u[r, :, ::16] = c * (0.9 + 0.1 * rng.random((128, 8, 4))) * 2.0 ** 30
        else: u[r, :, ::16] = c * (1.0 + 0.125 * rng.integers(0, 8, (128, 8, 4))) * 2.0 ** -30
        if o[r] < 2: v[r] = (0.9 + 0.1 * rng.random((128, 512))) * 2.0 ** 30
        else: v[r] = (1.0 + 0.125 * rng.integers(0, 8, (128, 512))) * 2.0 ** -30
        v[r] *= rng.choice([-1.0, 1.0], (128, 512))
        k = np.full(128, 32.0)
        if o[r] == 3: k = np.where(i < 120, 2.0 ** -8, 2.0 ** 8)
        for b in range(4): w[r, i, b, i, b] = k
    return {"x": x.astype(np.float32).reshape(N, 128, 4 * C).astype(BF), "u": u.reshape(N, 128, 512).astype(BF), "v": v.astype(BF), **stored(e), **weights(rng, w.astype(BF))}
def setup_inputs_spread(rng):
    d = setup_inputs(rng)
    d["x"] = wide(rng, N, 128, 4 * C, cols=6)
    return d
def check_inputs(d):
    b = []
    for k in ("x", "u", "v"):
        a = np.abs(d[k].astype(np.float32))
        if not (np.isfinite(a).all() and ((a == 0) | (a >= 2.0 ** -30) & (a <= 2.0 ** 30)).all()): b.append("a value of " + k)
    if not ((d["nx"] >= 0) & (d["nx"] < C)).all(): b.append("an entry of nx")
    else:
        e = np.concatenate([gentries(d["nx"][r]) for r in range(N)])
        at, back = np.zeros(8 * N, np.int64), np.zeros(8 * N, np.int64)
        for i in range(1, C + 1):
            at = e[np.arange(8 * N), at]
            back = np.where((at == 0) & (back == 0), i, back)
        if not (back == C).all(): b.append("a ring of nx")
    none, least, most = [emit(mx_ref.quantize(np.full((128, 16), k, np.float32).astype(BF)))[1][0, 0] for k in (0.0, 2.0 ** -8, 2.0 ** 8)]
    for r in range(N):
        if ((d["wc"][r] == 0x7F) | (d["wc"][r] == 0xFF)).any(): b.append("wc: a code that is no number")
        s = mx_ref.live(d["ws"][r])
        if ((s != none) & ((s < least) | (s > most))).any(): b.append("ws: a scale out of range")
    return b
def at(a, e):
    return np.take_along_axis(a, e, axis=1)
def mean(a, b):
    return ((a.astype(np.float32) + b.astype(np.float32)) * np.float32(0.5)).astype(BF)
def reference(x, u, v, nx, wc, ws):
    qu = [mx_ref.quantize(u[r]) for r in range(N)]
    lay = [pk(wc[r], ws[r]) for r in range(N)]
    ring = [gentries(nx[r]).astype(np.int64) for r in range(N)]
    now = [x[r] for r in range(N)]
    for m in MASK:
        t, new, back, z = [], [], [], []
        for r in range(N):
            q = mx_ref.quantize(now[r])
            t.append(decode(q).astype(BF))
            up = mx_ref.matmul(qu[r], q)[::16] > 0
            guest = ring[r ^ m]
            host = np.argsort(guest, axis=1)
            leave = up & ~at(up, host)
            a = ring[r]
            for i in range(8):
                a = np.where(at(leave, a), at(a, a), a)
            new.append(np.where(leave, at(a, host), np.where(at(leave, guest), guest, a)))
            back.append(np.argsort(new[r], axis=1))
            z.append(mx_ref.quantize(mean(gcols(t[r], new[r]), gcols(t[r], back[r]))))
        for r in range(N):
            h = tile([mx_ref.matmul(pick(lay[r], np.arange(128 * b, 128 * b + 128)), z[r ^ m]) * np.float32(0.03125) for b in range(4)])
            now[r] = mean(gcols(t[r], back[r]), gcols(h, new[r]))
        ring = new
    y, nr = np.zeros((N, 128, C), np.float32), np.zeros((N, 8, C), np.float32)
    oc, osc = np.zeros((N, 128, 4 * C), np.uint8), np.zeros((N, 16, C), np.uint8)
    for r in range(N):
        q = mx_ref.quantize(now[r])
        y[r] = mx_ref.matmul(mx_ref.quantize(v[r]), q)
        nr[r] = ring[r]
        oc[r], osc[r] = emit(q)
    return {"y": y, "nr": nr, "oc": oc, "osc": osc}

@@ -1,0 +1,426 @@
+from concourse.mybir import dt, AluOpType, AxisListType, ActivationFunctionType
+
+N, C, MASK = 8, 320, [4, 1, 2]
+BF, F4, I4, U2, CO, PL = "bfloat16", "float32", "int32", "uint16", "float8_e4m3fn_x4", "uint8"
+POW = [1, 2, 3, 4, 8, 12, 16, 32, 48, 64]
+SCRATCH = {}
+
+
+def _sb(dtype, **kw):
+    for k, n in kw.items():
+        SCRATCH[k] = ("sbuf", [128, n], dtype)
+
+
+_sb(I4, nxi=20, rnx=20, jp=C, jpa=C, c16=8, di=40, da=40)
+_sb(BF, xin=4 * C, ut=512, vt=512, xt=4 * C, zt=4 * C, tb=4 * C, tp=4 * C, hb=4 * C, gb=4 * C, zb=4 * C,
+    M=C, rst=C, iotac=C, zero=2 * C, low0=48, low1=48, og=48, ones=516, ef=516, rk=len(POW) * C, pm0=C, pm1=C, sc0=C, sc1=C,
+    hr=C, posr=C, ordr=C, uu=C, sg=C, svc=C, gsv=C, lvs=C, d3=C, th3=16, dR=C, iotaT=C, phr=C, vf=2 * C, nvf=2 * C, cb=656)
+_sb(F4, dI=16, mP=16, wn=16, wn2=1, wc0=C, wc1=C, jf=C, jS=C, KE=C, KO=C, M20=C, ov=2, of=3, nb=2, thr=1, lv=20, pos2=20, dq=20, ph2=20, t1=20, t2=20,
+    gS=C, cap=2 * C, fi=1296, wr=2, xm=2 * C, xsc=2 * C, rst2=2 * C, nrr=C, yo=C)
+_sb(U2, lk=60, ou=2, ou1=2, ol=20, gl=20, hl=20, ql=20, pu=20, ul=8)
+for _r in range(3):
+    _sb(U2, **{"lab%d" % _r: 40, "rlab%d" % _r: 40})
+    _sb(CO, **{"rq%d" % _r: C})
+    _sb(PL, **{"rs%d" % _r: C})
+    if _r: _sb(U2, **{"glab%d" % _r: 40})
+for _r in range(4):
+    _sb(CO, **{"xq%d" % _r: C})
+    _sb(PL, **{"xs%d" % _r: C})
+_sb(CO, zq=C, uq=128, uw=128, vq=128, wq=512, eq=512)
+_sb(PL, zs=C, us=128, uws=128, vs=128, wsb=512, es=512)
+for _r in range(8):
+    SCRATCH["ps%d" % _r] = ("psum", [128, 512], F4)
+SEMAPHORES = ["cv", "ct", "ca", "cg", "d_nx", "d_x", "d_u", "d_wc", "d_ws", "d_v", "d_out", "sent", "r_nx"] + \
+    ["r_x%d" % r for r in range(3)] + ["r_l%d" % r for r in range(3)] + ["r_g%d" % r for r in (1, 2)]
+
+
+def rank_program(g, core, T, topo):
+    rank = T.rank_of(core)
+    if rank is None:
+        return
+    A, ACT = AluOpType, ActivationFunctionType
+    ve, te, sc, sy = g.vector, g.tensor, g.scalar, g.sync
+    Q = {"v": ve, "t": te, "a": sc, "g": g, "s": sy}
+    count = {}
+    clock = {q: {} for q in Q}
+    wrote, read = {}, {}
+
+    def need(q, tok):
+        name, val, snap = tok
+        if clock[q].get(name, 0) < val:
+            Q[q].wait_ge(T.sem[name], val)
+            for k, v in list(snap.items()) + [(name, val)]:
+                clock[q][k] = max(clock[q].get(k, 0), v)
+
+    def waits(q, rd, wr):
+        toks = [wrote[k] for k in rd]
+        for k in wr:
+            if k in wrote: toks.append(wrote[k])
+            toks += read.get(k, [])
+        best = {}
+        for t in toks:
+            if t[0] not in best or best[t[0]][1] < t[1]: best[t[0]] = t
+        for t in best.values(): need(q, t)
+
+    def op(q, fn, rd, wr, sem=None, inc=1):
+        rd, wr = rd.split(), wr.split()
+        waits(q, rd, wr)
+        sem = sem or "c" + q
+        count[sem] = count.get(sem, 0) + inc
+        fn().then_inc(T.sem[sem], inc)
+        tok = (sem, count[sem], dict(clock[q]))
+        for k in rd: read.setdefault(k, []).append(tok)
+        for k in wr: wrote[k], read[k] = tok, []
+        return tok
+
+    def dma(q, out, in_, sem, rd, wr):
+        return op(q, lambda: Q[q].dma_start(out, in_), rd, wr, sem, 16)
+
+    def send(dst, pieces, rsem, rd):
+        waits("g", rd.split(), [])
+        rid, pid = topo.addr(dst, core)
+        mask, n = topo.mask(core, dst), len(topo.engines(core, dst))
+        for out, in_ in pieces:
+            g.remote_dma(out, in_, T.sem[rsem], T.sem.sent, pid, rid, mask)
+            count["sent"] = count.get("sent", 0) + n
+            count[rsem] = count.get(rsem, 0) + n
+
+    def landed(rsem, val, wr):
+        for k in wr.split(): wrote[k] = (rsem, val, {})
+
+    partner = [T.cores[rank ^ m] for m in MASK]
+    NE = len(topo.engines(core, partner[0]))
+    TT = lambda out, a, b, o, rd, wr: op("v", lambda: ve.tensor_tensor(out, a, b, o), rd, wr)
+    TS = lambda out, a, s1, s2, o, o2, rd, wr: op("v", (lambda: ve.tensor_scalar(out, a, s1, s2, o, o2)) if o2 is not None else (lambda: ve.tensor_scalar(out, a, s1, None, o)), rd, wr)
+    TC = lambda out, a, rd, wr: op("v", lambda: ve.tensor_copy(out, a), rd, wr)
+    SCAN = lambda out, a, b, i, o, o2, rd, wr: op("v", lambda: ve.tensor_tensor_scan(out, a, b, i, o, o2), rd, wr)
+    MS = lambda ap, c, wr: op("v", lambda: ve.memset(ap, c), "", wr)
+    AC = lambda out, a, rd, wr, scale=1.0: op("a", lambda: sc.activation(out, a, ACT.Copy, scale=scale), rd, wr)
+    ID = lambda out, a, bias, scale, rd, wr: op("a", lambda: sc.activation(out, a, ACT.Identity, bias=bias, scale=scale), rd, wr)
+    QZ = lambda q, s, t, rd, wr: op("v", lambda: ve.quantize_mx(q, s, t), rd, wr)
+    MM = lambda ps, l, ls, m, ms, rd, wr: op("t", lambda: te.matmul_mx(ps, l, ls, m, ms, True, True), rd, wr)
+    PLN = lambda buf, b: buf[:, C * b:C * b + C]
+    turn = [0]
+
+    dma("s", T.nxi[:, :], T.nx[:, :], "d_nx", "", "nxi")
+    dma("s", T.xin[:, :], T.x[:, :], "d_x", "", "xin")
+    dma("s", T.ut[:, :], T.u[:, :], "d_u", "", "ut")
+    dma("s", T.wq[:, :].bitcast(dt.uint8), T.wc[:, :], "d_wc", "", "wq")
+    dma("s", T.wsb[:, :], T.ws[:, :], "d_ws", "", "wsb")
+    dma("s", T.vt[:, :], T.v[:, :], "d_v", "", "vt")
+
+    op("g", lambda: g.iota(T.jp[:, :], [[0, 20], [1, 16]], 0, -1), "", "jp")
+    op("g", lambda: g.iota(T.iotac[:, :], [[1, C]], -160, 0, allow_small_or_imprecise_dtypes=True), "", "iotac")
+    send(partner[0], [(T.rnx[:, :], T.nxi[:, :])], "r_nx", "nxi")
+    landed("r_nx", NE, "rnx")
+    MS(T.ones[:, :], 1.0, "ones")
+    op("g", lambda: g.affine_select(T.ef[:, :], T.ones[:, :], [[-1, 516]], A.is_equal, 0.0, 3, 4), "ones", "ef")
+    op("g", lambda: g.iota(T.c16[:, :], [[16, 8]], 0, 0), "", "c16")
+    MS(T.rst[:, :], 1.0, "rst")
+    MS(T.rst[:, 0:C:16], 0.0, "rst")
+    op("g", lambda: g.iota(T.jf[:, :], [[1, C]], 0, 0, allow_small_or_imprecise_dtypes=True), "", "jf")
+    MS(T.of[:, 0:1], -160.0 * 2.0 ** -96, "of0")
+    MS(T.ou[:, :], 0, "ou")
+    MS(T.zero[:, :], 0.0, "zero")
+    MS(T.low0[:, :], 0.0, "low0")
+    MS(T.low1[:, :], 0.0, "low1")
+    TS(T.jpa[:, :], T.jp[:, :], 15, None, A.bitwise_and, None, "jp", "jpa")
+    TS(T.M[:, :], T.jpa[:, :], 0.0, None, A.is_equal, None, "jpa", "M")
+
+    fillers = []
+
+    def gap(n=1):
+        for _ in range(n):
+            if fillers: fillers.pop(0)()
+
+    def conv(pieces, finish):
+        b = turn[0] = 1 - turn[0]
+        pm, s, kp, ks = T["pm%d" % b], T["sc%d" % b], "pm%d" % b, "sc%d" % b
+        at, keys = 0, []
+        for i, (win, off, rd, n) in enumerate(pieces):
+            k = kp if i == 0 else "%s_%d" % (kp, i)
+            TT(pm[:, at:at + n], win.indirect(off), T.M[:, 0:n], A.mult, rd + " M", kp if i == 0 else k)
+            keys.append(k)
+            at += n
+        gap()
+        SCAN(s[:, 0:at], T.rst[:, 0:at], pm[:, 0:at], 0.0, A.mult, A.add, " ".join(keys) + " rst", ks)
+        gap()
+        finish(s[:, 15:at:16], ks)
+        gap()
+
+    S96, P96 = 2.0 ** -96, 2.0 ** 96
+
+    def to_list(out, wr):
+        return lambda v, k: TS(out, v, P96, 160.0, A.mult, A.add, k, wr)
+
+    def weigh(src, rd, finish):
+        b = turn[0] = 1 - turn[0]
+        w, k = T["wc%d" % b], "wc%d" % b
+        SCAN(w[:, :], T.dR[:, :], src, 0.0, A.mult, A.add, rd + " dR", k)
+        gap()
+        finish(w[:, 15:C:16], k)
+        gap()
+
+    def to_wlist(out, wr):
+        return lambda v, k: TS(out, v, T.wn[:, 15:16], 160.0, A.mult, A.add, k + " wn", wr)
+
+    RK = {m: T.rk[:, C * i:C * i + C] for i, m in enumerate(POW)}
+    LK = {m: T.lk[:, 20 * i:20 * i + 20] for i, m in enumerate([1, 4, 16])}
+    OLALL = "ol0 ol1 ol2 ol3 ol4 ol5"
+
+    def times(m, by):
+        AC(RK[m + by], RK[m].indirect(LK[by]), "rk%d lk%d" % (m, by), "rk%d" % (m + by))
+
+    def listed(m):
+        weigh(RK[m], "rk%d" % m, to_wlist(LK[m], "lk%d" % m))
+
+    def digit(l, d, m, lst, k):
+        TT(T.og[:, 16 * d - 16:16 * d], RK[m].indirect(lst), T["low%d" % l][:, 16 * d - 16:16 * d], A.mult, "rk%d low%d " % (m, l) + k, "og%d" % d)
+
+    def digits(l, out, wr):
+        op("v", lambda: ve.tensor_reduce(T.ov[:, l:l + 1], T.og[:, :], AxisListType.X, A.add), "og1 og2 og3", "ov%d" % l)
+        gap()
+        TS(T.of[:, l + 1:l + 2], T.of[:, l:l + 1], T.nb[:, l:l + 1], T.ov[:, l:l + 1], A.mult, A.add, "of%d nb%d ov%d" % (l, l, l), "of%d" % (l + 1))
+        gap()
+        TS(out, T.of[:, l + 1:l + 2], P96, 160.0, A.mult, A.add, "of%d" % (l + 1), wr)
+
+    def xname(r): return T["xq%d" % r], T["xs%d" % r], "xq%d" % r
+
+    def quant_x(r):
+        q, s, k = xname(r)
+        t, tk = (T.xin, "xin") if r == 0 else (T.xt, "xt0 xt1 xt2 xt3")
+        QZ(q[:, :], s[:, :], t[:, :], tk, k)
+
+    def quant_e(b):
+        QZ(T.eq[:, 128 * b:128 * b + 128], T.es[:, 128 * b:128 * b + 128], T.ef[:, 3 - b:515 - b], "ef", "eq%d" % b)
+
+    def spread(r, q, s, k, banks):
+        for b in range(4):
+            MM(T["ps%d" % banks[b]][:, 0:C], T.eq[:, 128 * b:128 * b + 128], T.es[:, 128 * b:128 * b + 128], q[:, :], s[:, :], "eq%d " % b + k, "ps%d" % banks[b])
+
+    NEAR, FAR = [1, 2, 3, 4], [5, 6, 7, 0]
+
+    def start(r):
+        q, s, k = xname(r)
+        send(partner[r], [(T["rq%d" % r][:, :].bitcast(dt.uint8), q[:, :].bitcast(dt.uint8)), (T["rs%d" % r][:, :], s[:, :])], "r_x%d" % r, k)
+        landed("r_x%d" % r, 2 * NE, "rq%d" % r)
+
+    def scores(r):
+        q, s, k = xname(r)
+        for p in (0, 7):
+            MM(T["ps%d" % p][:, 0:C], T.uw[:, :], T.uws[:, :], q[:, :], s[:, :], "uw " + k, "ps%d" % p)
+
+    def unpack(b):
+        AC(PLN(T.tb, b), T["ps%d" % NEAR[b]][:, 0:C], "ps%d" % NEAR[b], "tb%d" % b, 0.5)
+
+    def unpack_far(r):
+        q, s, k = T["rq%d" % r], T["rs%d" % r], "rq%d" % r
+        spread(r, q, s, k, FAR)
+        for b in range(4):
+            AC(PLN(T.tp, b), T["ps%d" % FAR[b]][:, 0:C], "ps%d" % FAR[b], "tp%d" % b, 0.5)
+
+    def guests(r):
+        if r == 0: return T.gl[:, :], T.hl[:, :], "gl", "hl"
+        return T["glab%d" % r][:, 0:20], T["glab%d" % r][:, 20:40], "glab%d" % r, "glab%d" % r
+
+    def f_u(r):
+        TS(T.uu[:, :], T.ps0[:, 0:C], 0.0, None, A.is_gt, None, "ps0", "uu")
+        op("a", lambda: sc.activation(T.sg[:, :], T.ps7[:, 0:C], ACT.Sign), "ps7", "sg")
+
+    def f_sv(r):
+        gL, hL, gk, hk = guests(r)
+        TT(T.svc[:, :], T.uu[:, :].indirect(hL), T.sg[:, :], A.is_ge, "uu sg " + hk, "svc")
+
+    def f_lv():
+        SCAN(T.lvs[:, :], T.d3[:, :], T.svc[:, :], 0.0, A.mult, A.add, "svc d3", "lvs")
+        gap()
+        TS(T.lv[:, :], T.lvs[:, 15:C:16], T.thr[:, 0:1], None, A.is_lt, None, "lvs thr", "lv")
+
+    TC(LK[1], T.nxi[:, :], "nxi", "lk1")
+    AC(RK[1], T.iotac[:, :].indirect(LK[1]), "iotac lk1", "rk1", S96)
+    for d in range(1, 4):
+        TC(T.low0[:, 16 * d - 16 + d:16 * d:4], T.M[:, d:16:4], "M", "low0")
+        TC(T.low1[:, 16 * d - 16 + 4 * d:16 * d - 12 + 4 * d], T.M[:, 4 * d:4 * d + 4], "M", "low1")
+    op("v", lambda: ve.tensor_reduce(T.nb[:, 0:1], T.M[:, 0:16:4], AxisListType.X, A.add), "M", "nb0")
+    op("v", lambda: ve.tensor_reduce(T.nb[:, 1:2], T.M[:, 0:4], AxisListType.X, A.add), "M", "nb1")
+    times(1, 1); times(2, 1); times(3, 1)
+    AC(T.iotaT[:, :], T.iotac[:, :], "iotac", "iotaT", S96)
+    TS(T.dR[:, :], T.M[:, :], -16384.0, 16384.0, A.mult, A.add, "M", "dR")
+    TS(T.dI[:, :], T.M[:, 0:16], -2.0 ** -14, 2.0 ** -14, A.mult, A.add, "M", "dI")
+    TS(T.mP[:, :], T.M[:, 0:16], P96, None, A.mult, None, "M", "mP")
+    digit(0, 1, 1, T.ou[:, 0:1], "ou")
+    SCAN(T.wn[:, :], T.dI[:, :], T.mP[:, :], 0.0, A.mult, A.add, "dI mP", "wn")
+    MS(T.cb[:, 0:1], -160.0, "cb0")
+    digit(0, 2, 2, T.ou[:, 0:1], "ou")
+    TS(T.wn2[:, :], T.wn[:, 15:16], 2.0, None, A.mult, None, "wn", "wn2")
+    TS(T.d3[:, :], T.M[:, :], -3.0, 3.0, A.mult, A.add, "M", "d3")
+    quant_e(0); quant_e(1)
+    digit(0, 3, 3, T.ou[:, 0:1], "ou")
+    quant_e(2); quant_e(3)
+    fillers += [lambda: TC(T.ul[:, :], T.c16[:, :], "c16", "ul"),
+                lambda: MS(T.fi[:, 0:1], 0.0, "fi0")]
+    listed(4)
+    times(4, 4); times(8, 4); times(12, 4)
+    fillers += [lambda: SCAN(T.th3[:, :], T.d3[:, 0:16], T.M[:, 0:16], 0.0, A.mult, A.add, "d3 M", "th3"),
+                lambda: MS(T.fi[:, 1287:1288], 1.0, "fi1")]
+    digits(0, T.ou1[:, 0:1], "ou1")
+    TS(T.thr[:, :], T.th3[:, 15:16], 0.75, None, A.mult, None, "th3", "thr")
+    digit(1, 1, 4, T.ou1[:, 0:1], "ou1")
+    quant_x(0)
+    start(0)
+    digit(1, 2, 8, T.ou1[:, 0:1], "ou1")
+    QZ(T.uq[:, :], T.us[:, :], T.ut[:, :], "ut", "uq")
+    TC(T.uw[:, :].bitcast(dt.uint32), T.uq[:, :].bitcast(dt.uint32).indirect(T.ul[:, :]), "uq ul", "uwc")
+    digit(1, 3, 12, T.ou1[:, 0:1], "ou1")
+    op("a", lambda: sc.activation(T.uws[:, :], T.us[:, :].indirect(T.ul[:, :]), ACT.Copy), "uq ul uwc", "uw")
+    listed(16)
+    scores(0)
+    times(16, 16); times(32, 16); times(48, 16)
+    fillers += [lambda: TC(T.gl[:, :], T.rnx[:, :], "rnx", "gl")]
+    digits(1, T.ol[:, 0:1], "ol0")
+    spread(0, T.xq0, T.xs0, "xq0", NEAR)
+    S20 = 2.0 ** -20
+    AC(T.jS[:, :], T.jf[:, :], "jf", "jS", S20)
+    ID(T.KE[:, :], T.jf[:, :], 641 * 512 * S20, 1024 * S20, "jf", "KE")
+    op("v", lambda: ve.tensor_copy(T.hr[:, :].indirect(T.gl[:, :]), T.iotaT[:, :]), "gl iotaT", "hr")
+    conv([(RK[16 * d], T.ol[:, 0:1], "rk%d ol0" % (16 * d), 16) for d in range(1, 4)], to_list(T.ol[:, 1:4], "ol1"))
+    for i in range(4):
+        if i == 0: fillers += [lambda: f_u(0)]
+        if i == 1: weigh(T.hr[:, :], "hr", to_wlist(T.hl[:, :], "hl"))
+        if i == 1:
+            ID(T.KO[:, :], T.jf[:, :], 642 * 512 * S20, 1024 * S20, "jf", "KO")
+            AC(T.M20[:, :], T.M[:, :], "M", "M20", 2.0 ** 20)
+            AC(T.rst2[:, 0:C], T.rst[:, :], "rst", "rst2a")
+        if i == 2: fillers += [lambda: f_sv(0)]
+        if i == 3: fillers += [lambda: f_lv()]
+        conv([(RK[64], T.ol[:, 4 * i:4 * i + 4], "rk64 " + ("ol0 ol1" if i == 0 else "ol%d" % (i + 1)), 64)], to_list(T.ol[:, 4 * i + 4:4 * i + 8], "ol%d" % (i + 2)))
+    gap(len(fillers))
+
+    def slots(r):
+        gL, hL, gk, hk = guests(r)
+        AC(T.gsv[:, :], T.svc[:, :].indirect(gL), "svc " + gk, "gsv")
+        (TC if r else AC)(T.vf[:, 0:2 * C:2], T.svc[:, :].indirect(T.ol[:, :]), "svc " + OLALL, "vfa")
+        ID(T.vf[:, 1:2 * C:2], T.gsv[:, :].indirect(T.ol[:, :]), 1.0, -1.0, "gsv " + OLALL, "vfb")
+
+    def holes():
+        ID(T.nvf[:, :], T.vf[:, :], 1.0, -1.0, "vfa vfb", "nvf")
+
+    def cap_even(): TT(T.cap[:, 0:2 * C:2], T.jS[:, :].indirect(T.ol[:, :]), T.KE[:, :], A.add, "jS KE " + OLALL, "capa")
+
+    def cap_odd(): TT(T.cap[:, 1:2 * C:2], T.gS[:, :].indirect(T.ol[:, :]), T.KO[:, :], A.add, "gS KO " + OLALL, "capb")
+
+    def guest_cols(r):
+        gL, hL, gk, hk = guests(r)
+        AC(T.gS[:, :], T.jS[:, :].indirect(gL), "jS " + gk, "gS")
+
+    def host_at(r):
+        gL, hL, gk, hk = guests(r)
+        AC(T.phr[:, :], T.posr[:, :].indirect(hL), "posr " + hk, "phr")
+
+    def host_place():
+
+        def fin(v, k):
+            TS(T.ph2[:, :], v, T.wn2[:, 0:1], 321.0, A.mult, A.add, k + " wn2", "ph2")
+            gap()
+            TT(T.dq[:, :], T.ph2[:, :], T.pos2[:, :], A.subtract, "ph2 pos2", "dq")
+        weigh(T.phr[:, :], "phr", fin)
+
+    slots(0)
+    op("v", lambda: ve.tensor_copy(T.posr[:, :].indirect(T.ol[:, :]), T.iotaT[:, :]), "iotaT " + OLALL, "posr")
+    host_at(0)
+    guest_cols(0)
+    holes()
+    AC(T.rst2[:, C:], T.rst[:, :], "rst", "rst2b")
+    for b in range(4): unpack(b)
+    fillers += [cap_even]
+    weigh(T.posr[:, :], "posr", lambda v, k: TS(T.pos2[:, :], v, T.wn2[:, 0:1], 320.0, A.mult, A.add, k + " wn2", "pos2"))
+    fillers += [cap_odd]
+    host_place()
+
+    for r in range(3):
+        lab, rlab, lk, rk = T["lab%d" % r], T["rlab%d" % r], "lab%d" % r, "rlab%d" % r
+        last = r == 2
+        if r:
+            quant_x(r)
+            start(r)
+            scores(r)
+            q, s, k = xname(r)
+            spread(r, q, s, k, NEAR)
+            cap_even()
+            f_u(r)
+            unpack(0)
+            f_sv(r)
+            slots(r)
+            holes()
+            fillers += [cap_odd]
+            f_lv()
+            gap(len(fillers))
+            unpack(1); unpack(2); unpack(3)
+        unpack_far(r)
+        TT(T.t1[:, :], T.lv[:, :], T.dq[:, :], A.mult, "lv dq", "t1")
+        TT(T.t2[:, :], T.t1[:, :], T.pos2[:, :], A.add, "t1 pos2", "t2")
+        SCAN(T.fi[:, 1:641], T.vf[:, :], T.cap[:, :], 0.0, A.max, A.min, "vfa vfb capa capb", "fif")
+        TC(T.ql[:, :], T.t2[:, :], "t2", "ql")
+        SCAN(T.fi[:, 1286:646:-1], T.nvf[:, ::-1], T.cap[:, ::-1], 1.0, A.min, A.max, "nvf capa capb", "fib")
+        TT(T.xm[:, C:], T.fi[:, 0:640].indirect(T.ql[:, :]), T.M20[:, :], A.mult, "fif fi0 ql M20", "xmb")
+        TT(T.xm[:, 0:C], T.fi[:, 648:1288].indirect(T.ql[:, :]), T.M20[:, :], A.mult, "fib fi1 ql M20", "xma")
+        TS(T.wr[:, :], T.fi[:, 640:648:7], 2.0 ** 20, None, A.mult, None, "fif fib", "wr")
+        SCAN(T.xsc[:, :], T.rst2[:, :], T.xm[:, :], 0.0, A.mult, A.add, "rst2a rst2b xma xmb", "xsc")
+        TS(T.di[:, 0:20], T.xsc[:, 15:C:16], -327680.0, T.wr[:, 1:2], A.add, A.min, "xsc wr", "dia")
+        TS(T.di[:, 20:40], T.xsc[:, C + 15:2 * C:16], 327680.0, T.wr[:, 0:1], A.add, A.max, "xsc wr", "dib")
+        TS(T.da[:, :], T.di[:, :], 511, None, A.bitwise_and, None, "dia dib", "da")
+        TC(lab[:, :], T.da[:, :], "da", lk)
+        send(partner[r], [(rlab[:, :], lab[:, :])], "r_l%d" % r, lk)
+        landed("r_l%d" % r, NE, rk)
+        if not last:
+            n = r + 1
+            send(partner[n], [(T["glab%d" % n][:, :], lab[:, :])], "r_g%d" % n, lk)
+            landed("r_g%d" % n, NE, "glab%d" % n)
+        a, b_, ra, rb = lab[:, 0:20], lab[:, 20:40], rlab[:, 0:20], rlab[:, 20:40]
+        def own_b(b): AC(PLN(T.gb, b), PLN(T.tb, b).indirect(b_), "tb%d " % b + lk, "gb%d" % b)
+
+        if not last:
+            SCAN(T.cb[:, 1:641], T.vf[:, :], T.zero[:, :], -160.0, A.add, A.add, "vfa vfb zero", "cb")
+            TS(T.posr[:, :], T.cb[:, 0:640].indirect(T.ql[:, :]), S96, None, A.mult, None, "cb cb0 ql", "posr")
+
+            def fin(v, k):
+                TS(T.pu[:, :], v, T.wn[:, 15:16], 160.0, A.mult, A.add, k + " wn", "pu")
+                TS(T.pos2[:, :], v, T.wn2[:, 0:1], 320.0, A.mult, A.add, k + " wn2", "pos2")
+            weigh(T.posr[:, :], "posr", fin)
+            op("v", lambda: ve.tensor_copy(T.ordr[:, :].indirect(T.pu[:, :]), T.iotaT[:, :]), "pu iotaT", "ordr")
+        for b in range(4): own_b(b)
+        if last:
+            QZ(T.vq[:, :], T.vs[:, :], T.vt[:, :], "vt", "vq")
+        AC(T.zb[:, 0:160], PLN(T.tp, 0).indirect(rlab[:, 20:30]), "tp0 " + rk, "zb0a")
+        TC(T.zb[:, 160:C], PLN(T.tp, 0).indirect(rlab[:, 30:40]), "tp0 " + rk, "zb0")
+        for b in range(1, 4):
+            AC(PLN(T.zb, b), PLN(T.tp, b).indirect(rb), "tp%d " % b + rk, "zb%d" % b)
+        for b in range(4):
+            TT(T.zt[:, b:4 * C:4], PLN(T.tp, b).indirect(ra), PLN(T.zb, b), A.add, "tp%d zb%d " % (b, b) + rk + (" zb0a" if b == 0 else ""), "zt%d" % b)
+        QZ(T.zq[:, :], T.zs[:, :], T.zt[:, :], "zt0 zt1 zt2 zt3", "zq")
+        for b in range(4):
+            MM(T["ps%d" % (b + 1)][:, 0:C], T.wq[:, 128 * b:128 * b + 128], T.wsb[:, 128 * b:128 * b + 128], T.zq[:, :], T.zs[:, :], "wq wsb zq", "ps%d" % (b + 1))
+        if not last:
+            host_at(r + 1)
+            weigh(T.ordr[:, :], "ordr", to_wlist(T.ol[:, :], OLALL))
+            host_place()
+        for b in range(4):
+            AC(PLN(T.hb, b), T["ps%d" % (b + 1)][:, 0:C], "ps%d" % (b + 1), "hb%d" % b, 2.0 ** -6)
+        for b in range(4):
+            TT(T.xt[:, b:4 * C:4], PLN(T.hb, b).indirect(a), PLN(T.gb, b), A.add, "hb%d gb%d " % (b, b) + lk, "xt%d" % b)
+        if not last:
+            guest_cols(r + 1)
+        else:
+            AC(T.nrr[:, :], T.jf[:, :].indirect(a), "jf " + lk, "nrr")
+            dma("s", T.nr[:, :], T.nrr[0:128:16, :], "d_out", "nrr", "nr")
+
+    q, s, k = xname(3)
+    quant_x(3)
+    MM(T.ps0[:, 0:C], T.vq[:, :], T.vs[:, :], q[:, :], s[:, :], "vq " + k, "ps0")
+    dma("s", T.oc[:, :], q[:, :].bitcast(dt.uint8), "d_out", k, "oc")
+    for i in range(4):
+        dma("a" if i % 2 else "s", T.osc[4 * i:4 * i + 4, :], s[32 * i:32 * i + 4, :], "d_out", k, "osc%d" % i)
+    TC(T.yo[:, :], T.ps0[:, 0:C], "ps0", "yo")
+    dma("s", T.y[:, :], T.yo[:, :], "d_out", "yo", "y")
+    for name in SEMAPHORES:
+        if count.get(name): need("s", (name, count[name], {}))

@@ -1,8 +1,12 @@
-from concourse.mybir import dt, AluOpType, AxisListType, ActivationFunctionType
+from concourse.mybir import dt, AluOpType, ActivationFunctionType
 
 N, C, MASK = 8, 320, [4, 1, 2]
 BF, F4, I4, U2, CO, PL = "bfloat16", "float32", "int32", "uint16", "float8_e4m3fn_x4", "uint8"
-POW = [1, 2, 3, 4, 8, 12, 16, 32, 48, 64]
+POW = [1, 2, 4, 8, 16, 32, 64]
+SPLIT = [8, 8, 8, 8, 8, 8, 8]
+PIECES = [(0, 192), (192, C)]
+FIRST = [(0, 256), (256, C)]
+HEAD = 337
 SCRATCH = {}
 
 
@@ -11,13 +15,13 @@ def _sb(dtype, **kw):
         SCRATCH[k] = ("sbuf", [128, n], dtype)
 
 
-_sb(I4, nxi=20, rnx=20, jp=C, jpa=C, c16=8, di=40, da=40)
+_sb(I4, nxi=20, jp=16, jpa=16)
 _sb(BF, xin=4 * C, ut=512, vt=512, xt=4 * C, zt=4 * C, tb=4 * C, tp=4 * C, hb=4 * C, gb=4 * C, zb=4 * C,
-    M=C, rst=C, iotac=C, zero=2 * C, low0=48, low1=48, og=48, ones=516, ef=516, rk=len(POW) * C, pm0=C, pm1=C, sc0=C, sc1=C,
-    hr=C, posr=C, ordr=C, uu=C, sg=C, svc=C, gsv=C, lvs=C, d3=C, th3=16, dR=C, iotaT=C, phr=C, vf=2 * C, nvf=2 * C, cb=656)
-_sb(F4, dI=16, mP=16, wn=16, wn2=1, wc0=C, wc1=C, jf=C, jS=C, KE=C, KO=C, M20=C, ov=2, of=3, nb=2, thr=1, lv=20, pos2=20, dq=20, ph2=20, t1=20, t2=20,
-    gS=C, cap=2 * C, fi=1296, wr=2, xm=2 * C, xsc=2 * C, rst2=2 * C, nrr=C, yo=C)
-_sb(U2, lk=60, ou=2, ou1=2, ol=20, gl=20, hl=20, ql=20, pu=20, ul=8)
+    ones=516, ef=516, minus=2 * C, iotac=C, iotaT=C, dR=C, dX=C, dR16=16, dX16=16, rk=len(POW) * C, ws_=8 * C, wo=C,
+    hr=C, gR=C, goR=C, posr=C, phr=C, ordr=C, w1=C, w2=C, lvc=C, svc=C, lcg=C, lvs=C, aR=C, bR=C,
+    nv=2 * C, d1=2 * C, ff=HEAD + 2 * C, fb=16 + 2 * C + HEAD, cb=2 * C + 16)
+_sb(F4, dI=16, mP=16, wn=16, wn2=1, c15=1, nc15=1, lv=20, sv=20, lw=20, l3=20, pos2=20, ph2=20, dq=20, kq=20, t0=20, t1=20, t2=20, nrr=C, yo=C)
+_sb(U2, lk=20 * len(POW), k16=20, inv=20, ol=20, gl=20, hl=20, go=20, ql=20, pu=20, ul=8)
 for _r in range(3):
     _sb(U2, **{"lab%d" % _r: 40, "rlab%d" % _r: 40})
     _sb(CO, **{"rq%d" % _r: C})
@@ -30,8 +34,46 @@ _sb(CO, zq=C, uq=128, uw=128, vq=128, wq=512, eq=512)
 _sb(PL, zs=C, us=128, uws=128, vs=128, wsb=512, es=512)
 for _r in range(8):
     SCRATCH["ps%d" % _r] = ("psum", [128, 512], F4)
-SEMAPHORES = ["cv", "ct", "ca", "cg", "d_nx", "d_x", "d_u", "d_wc", "d_ws", "d_v", "d_out", "sent", "r_nx"] + \
+SEMAPHORES = ["cv", "ct", "ca", "cg", "d_nx", "d_x", "d_u", "d_wc", "d_ws", "d_v", "d_out", "sent", "r_nx", "r_h"] + \
     ["r_x%d" % r for r in range(3)] + ["r_l%d" % r for r in range(3)] + ["r_g%d" % r for r in (1, 2)]
+
+CYCLE, GATHER, SCATTER, WAIT, LOAD, CALL, FLIGHT, BYTE = 0.95e-3, 1.56, 3.8, 0.12, 1.8, 0.25, 2.6, 1.5e-3
+PASSES, ORDER = 6, []
+
+
+def in_order(calls):
+    n = len(calls)
+    ahead, after = [c["deps"] for c in calls], [[] for c in calls]
+    for i in range(n):
+        for d in ahead[i]: after[d].append(i)
+
+    def place(order, before):
+        start, busy = {}, {}
+        for i in order:
+            c = calls[i]
+            lead = 0.0 if before is ahead else c["time"] - c["hold"]
+            t = max([0.0] + [start[d] + calls[d]["time"] + WAIT for d in before[i]])
+            if c["q"] is not None:
+                taken = busy.setdefault(c["q"], [])
+                for lo, hi in taken:
+                    if hi > t + lead + 1e-9 and lo < t + lead + c["hold"] - 1e-9: t = hi - lead
+                taken.append((t + lead, t + lead + c["hold"]))
+                taken.sort()
+            start[i] = t
+        return start
+
+    tail = [c["time"] for c in calls]
+    for i in range(n - 1, -1, -1):
+        for d in ahead[i]: tail[d] = max(tail[d], calls[d]["time"] + WAIT + tail[i])
+    best = None
+    for order in (list(range(n)), sorted(range(n), key=lambda i: -tail[i])):
+        for _ in range(PASSES):
+            start = place(order, ahead)
+            end = max(start[i] + calls[i]["time"] for i in range(n))
+            if best is None or end < best[0]: best = (end, sorted(range(n), key=lambda i: (start[i], i)))
+            back = place(sorted(range(n), key=lambda i: (-start[i] - calls[i]["time"], -i)), after)
+            order = sorted(range(n), key=lambda i: (-back[i] - calls[i]["time"], i))
+    return best[1]
 
 
 def rank_program(g, core, T, topo):
@@ -41,386 +83,273 @@ def rank_program(g, core, T, topo):
     A, ACT = AluOpType, ActivationFunctionType
     ve, te, sc, sy = g.vector, g.tensor, g.scalar, g.sync
     Q = {"v": ve, "t": te, "a": sc, "g": g, "s": sy}
-    count = {}
-    clock = {q: {} for q in Q}
-    wrote, read = {}, {}
+    calls, wrote, read = [], {}, {}
 
-    def need(q, tok):
-        name, val, snap = tok
-        if clock[q].get(name, 0) < val:
-            Q[q].wait_ge(T.sem[name], val)
-            for k, v in list(snap.items()) + [(name, val)]:
-                clock[q][k] = max(clock[q].get(k, 0), v)
+    def op(q, fn, rd, wr, time, sem=None, inc=1, hold=None):
+        rd, wr, i = rd.split(), wr.split(), len(calls)
+        deps = [wrote[k] for k in rd]
+        for k in wr: deps += read.get(k, []) + ([wrote[k]] if k in wrote else [])
+        calls.append({"q": q, "fn": fn, "deps": sorted(set(deps)), "time": time, "hold": time if hold is None else hold, "sem": sem or "c" + q, "inc": inc})
+        for k in rd: read.setdefault(k, []).append(i)
+        for k in wr: wrote[k], read[k] = i, []
 
-    def waits(q, rd, wr):
-        toks = [wrote[k] for k in rd]
-        for k in wr:
-            if k in wrote: toks.append(wrote[k])
-            toks += read.get(k, [])
-        best = {}
-        for t in toks:
-            if t[0] not in best or best[t[0]][1] < t[1]: best[t[0]] = t
-        for t in best.values(): need(q, t)
+    def dma(q, out, in_, sem, rd, wr, kb=0):
+        op(q, lambda: Q[q].dma_start(out, in_), rd, wr, LOAD + kb / 200, sem, 16, 0.05)
 
-    def op(q, fn, rd, wr, sem=None, inc=1):
-        rd, wr = rd.split(), wr.split()
-        waits(q, rd, wr)
-        sem = sem or "c" + q
-        count[sem] = count.get(sem, 0) + inc
-        fn().then_inc(T.sem[sem], inc)
-        tok = (sem, count[sem], dict(clock[q]))
-        for k in rd: read.setdefault(k, []).append(tok)
-        for k in wr: wrote[k], read[k] = tok, []
-        return tok
-
-    def dma(q, out, in_, sem, rd, wr):
-        return op(q, lambda: Q[q].dma_start(out, in_), rd, wr, sem, 16)
-
-    def send(dst, pieces, rsem, rd):
-        waits("g", rd.split(), [])
+    def send(dst, pieces, rsem, rd, wr, width):
         rid, pid = topo.addr(dst, core)
         mask, n = topo.mask(core, dst), len(topo.engines(core, dst))
-        for out, in_ in pieces:
-            g.remote_dma(out, in_, T.sem[rsem], T.sem.sent, pid, rid, mask)
-            count["sent"] = count.get("sent", 0) + n
-            count[rsem] = count.get(rsem, 0) + n
 
-    def landed(rsem, val, wr):
-        for k in wr.split(): wrote[k] = (rsem, val, {})
+        def fn():
+            for out, in_ in pieces: g.remote_dma(out, in_, T.sem[rsem], T.sem.sent, pid, rid, mask)
+        op("g", fn, rd, "gone_" + rsem, CALL * len(pieces), "sent", n * len(pieces))
+        op(None, None, "gone_" + rsem, wr, FLIGHT + BYTE * width, rsem, n * len(pieces))
 
+    def cost(n, rate): return max(64, n * rate) * CYCLE
+    def picked(n, rate=GATHER): return 0.06 + n * rate * CYCLE
+    def keys(name, lo, hi, step): return " ".join(name + str(i) for i in range(lo // step, (hi - 1) // step + 1))
+
+    TT = lambda out, a, b, o, rd, wr, t=cost(0, 0): op("v", lambda: ve.tensor_tensor(out, a, b, o), rd, wr, t)
+    TS = lambda out, a, s1, s2, o, o2, rd, wr, t=cost(0, 0): op("v", (lambda: ve.tensor_scalar(out, a, s1, s2, o, o2)) if o2 is not None else (lambda: ve.tensor_scalar(out, a, s1, None, o)), rd, wr, t)
+    TC = lambda out, a, rd, wr, t=cost(0, 0): op("v", lambda: ve.tensor_copy(out, a), rd, wr, t)
+    SCAN = lambda out, a, b, i, o, o2, rd, wr, n: op("v", lambda: ve.tensor_tensor_scan(out, a, b, i, o, o2), rd, wr, cost(n, 0.5))
+    MS = lambda ap, c, wr, n=0: op("v", lambda: ve.memset(ap, c), "", wr, cost(n, 0.5))
+    AC = lambda out, a, rd, wr, t, scale=1.0: op("a", lambda: sc.activation(out, a, ACT.Copy, scale=scale), rd, wr, t)
+    AF = lambda f, out, a, bias, scale, rd, wr, t: op("a", lambda: sc.activation(out, a, f, bias=bias, scale=scale), rd, wr, t)
+    QZ = lambda q, s, t, rd, wr, n: op("v", lambda: ve.quantize_mx(q, s, t), rd, wr, 0.014 + n * 1e-3)
+    MM = lambda ps, l, ls, m, ms, rd, wr, n: op("t", lambda: te.matmul_mx(ps, l, ls, m, ms, True, True), rd, wr, (n + 16) * 0.9e-3)
+    PLN = lambda buf, b, lo=0, hi=C: buf[:, C * b + lo:C * b + hi]
+    plain = lambda n: 0.06 + n * CYCLE
+    GC = lambda q, out, a, rd, wr, n: AC(out, a, rd, wr, picked(n)) if q == "a" else TC(out, a, rd, wr, picked(n))
+    S96, P96 = 2.0 ** -96, 2.0 ** 96
     partner = [T.cores[rank ^ m] for m in MASK]
-    NE = len(topo.engines(core, partner[0]))
-    TT = lambda out, a, b, o, rd, wr: op("v", lambda: ve.tensor_tensor(out, a, b, o), rd, wr)
-    TS = lambda out, a, s1, s2, o, o2, rd, wr: op("v", (lambda: ve.tensor_scalar(out, a, s1, s2, o, o2)) if o2 is not None else (lambda: ve.tensor_scalar(out, a, s1, None, o)), rd, wr)
-    TC = lambda out, a, rd, wr: op("v", lambda: ve.tensor_copy(out, a), rd, wr)
-    SCAN = lambda out, a, b, i, o, o2, rd, wr: op("v", lambda: ve.tensor_tensor_scan(out, a, b, i, o, o2), rd, wr)
-    MS = lambda ap, c, wr: op("v", lambda: ve.memset(ap, c), "", wr)
-    AC = lambda out, a, rd, wr, scale=1.0: op("a", lambda: sc.activation(out, a, ACT.Copy, scale=scale), rd, wr)
-    ID = lambda out, a, bias, scale, rd, wr: op("a", lambda: sc.activation(out, a, ACT.Identity, bias=bias, scale=scale), rd, wr)
-    QZ = lambda q, s, t, rd, wr: op("v", lambda: ve.quantize_mx(q, s, t), rd, wr)
-    MM = lambda ps, l, ls, m, ms, rd, wr: op("t", lambda: te.matmul_mx(ps, l, ls, m, ms, True, True), rd, wr)
-    PLN = lambda buf, b: buf[:, C * b:C * b + C]
     turn = [0]
 
+    def weigh(src, rd):
+        b = turn[0] = (turn[0] + 1) % 8
+        SCAN(T.ws_[:, C * b:C * b + C], T.dR[:, :], src, 0.0, A.mult, A.add, rd + " dR", "ws_%d" % b, C)
+        return T.ws_[:, C * b + 15:C * b + C:16], "ws_%d" % b
+
+    def listed(out, wr, v, k): TS(out, v, T.wn[:, 15:16], 160.0, A.mult, A.add, k + " wn", wr)
+
     dma("s", T.nxi[:, :], T.nx[:, :], "d_nx", "", "nxi")
-    dma("s", T.xin[:, :], T.x[:, :], "d_x", "", "xin")
-    dma("s", T.ut[:, :], T.u[:, :], "d_u", "", "ut")
-    dma("s", T.wq[:, :].bitcast(dt.uint8), T.wc[:, :], "d_wc", "", "wq")
-    dma("s", T.wsb[:, :], T.ws[:, :], "d_ws", "", "wsb")
-    dma("s", T.vt[:, :], T.v[:, :], "d_v", "", "vt")
+    dma("s", T.ut[:, :], T.u[:, :], "d_u", "", "ut", 131)
+    dma("s", T.xin[:, :], T.x[:, :], "d_x", "", "xt00 xt01 xt02 xt03 xt10 xt11 xt12 xt13", 460)
+    dma("s", T.wq[:, :].bitcast(dt.uint8), T.wc[:, :], "d_wc", "", "wq", 720)
+    dma("s", T.wsb[:, :], T.ws[:, :], "d_ws", "", "wsb", 790)
+    dma("s", T.vt[:, :], T.v[:, :], "d_v", "", "vt", 920)
 
-    op("g", lambda: g.iota(T.jp[:, :], [[0, 20], [1, 16]], 0, -1), "", "jp")
-    op("g", lambda: g.iota(T.iotac[:, :], [[1, C]], -160, 0, allow_small_or_imprecise_dtypes=True), "", "iotac")
-    send(partner[0], [(T.rnx[:, :], T.nxi[:, :])], "r_nx", "nxi")
-    landed("r_nx", NE, "rnx")
-    MS(T.ones[:, :], 1.0, "ones")
-    op("g", lambda: g.affine_select(T.ef[:, :], T.ones[:, :], [[-1, 516]], A.is_equal, 0.0, 3, 4), "ones", "ef")
-    op("g", lambda: g.iota(T.c16[:, :], [[16, 8]], 0, 0), "", "c16")
-    MS(T.rst[:, :], 1.0, "rst")
-    MS(T.rst[:, 0:C:16], 0.0, "rst")
-    op("g", lambda: g.iota(T.jf[:, :], [[1, C]], 0, 0, allow_small_or_imprecise_dtypes=True), "", "jf")
-    MS(T.of[:, 0:1], -160.0 * 2.0 ** -96, "of0")
-    MS(T.ou[:, :], 0, "ou")
-    MS(T.zero[:, :], 0.0, "zero")
-    MS(T.low0[:, :], 0.0, "low0")
-    MS(T.low1[:, :], 0.0, "low1")
+    MS(T.ones[:, :], 1.0, "ones", 516)
+    op("g", lambda: g.iota(T.jp[:, :], [[1, 16]], 0, -1), "", "jp", 0.13 + cost(16, 2))
+    op("g", lambda: g.affine_select(T.ef[:, :], T.ones[:, :], [[-1, 516]], A.is_equal, 0.0, 3, 4), "ones", "ef", 0.17 + cost(516, 2))
+    SCAN(T.iotac[:, :], T.ones[:, 0:C], T.ones[:, 0:C], -161.0, A.mult, A.add, "ones", "iotac", C)
+    TS(T.iotaT[:, :], T.iotac[:, :], S96, None, A.mult, None, "iotac", "iotaT", cost(C, 0.5))
+    MS(T.iotaT[:, 160:161], S96 * 2.0 ** -20, "iotaT")
     TS(T.jpa[:, :], T.jp[:, :], 15, None, A.bitwise_and, None, "jp", "jpa")
-    TS(T.M[:, :], T.jpa[:, :], 0.0, None, A.is_equal, None, "jpa", "M")
-
-    fillers = []
-
-    def gap(n=1):
-        for _ in range(n):
-            if fillers: fillers.pop(0)()
-
-    def conv(pieces, finish):
-        b = turn[0] = 1 - turn[0]
-        pm, s, kp, ks = T["pm%d" % b], T["sc%d" % b], "pm%d" % b, "sc%d" % b
-        at, keys = 0, []
-        for i, (win, off, rd, n) in enumerate(pieces):
-            k = kp if i == 0 else "%s_%d" % (kp, i)
-            TT(pm[:, at:at + n], win.indirect(off), T.M[:, 0:n], A.mult, rd + " M", kp if i == 0 else k)
-            keys.append(k)
-            at += n
-        gap()
-        SCAN(s[:, 0:at], T.rst[:, 0:at], pm[:, 0:at], 0.0, A.mult, A.add, " ".join(keys) + " rst", ks)
-        gap()
-        finish(s[:, 15:at:16], ks)
-        gap()
-
-    S96, P96 = 2.0 ** -96, 2.0 ** 96
-
-    def to_list(out, wr):
-        return lambda v, k: TS(out, v, P96, 160.0, A.mult, A.add, k, wr)
-
-    def weigh(src, rd, finish):
-        b = turn[0] = 1 - turn[0]
-        w, k = T["wc%d" % b], "wc%d" % b
-        SCAN(w[:, :], T.dR[:, :], src, 0.0, A.mult, A.add, rd + " dR", k)
-        gap()
-        finish(w[:, 15:C:16], k)
-        gap()
-
-    def to_wlist(out, wr):
-        return lambda v, k: TS(out, v, T.wn[:, 15:16], 160.0, A.mult, A.add, k + " wn", wr)
+    TS(T.dR16[:, :], T.jpa[:, :], 0.0, 16384.0, A.not_equal, A.mult, "jpa", "dR16")
+    TS(T.nc15[:, :], T.jpa[:, 15:16], -1.0, None, A.mult, None, "jpa", "nc15")
+    TS(T.k16[:, :], T.ones[:, 0:20], T.nc15[:, 0:1], 15.0, A.mult, A.add, "ones nc15", "k16")
+    GC("a", T.dR[:, :], T.dR16[:, :].indirect(T.k16[:, :]), "dR16 k16", "dR", C)
+    AF(ACT.Identity, T.dX[:, :], T.dR[:, :], -256.0, 257.0 / 16384.0, "dR", "dX", plain(C))
+    TS(T.dI[:, :], T.dR16[:, :], 2.0 ** -28, None, A.mult, None, "dR16", "dI")
+    TS(T.mP[:, :], T.jpa[:, :], 0.0, P96, A.is_equal, A.mult, "jpa", "mP")
+    SCAN(T.wn[:, :], T.dI[:, :], T.mP[:, :], 0.0, A.mult, A.add, "dI mP", "wn", 0)
+    TS(T.wn2[:, :], T.wn[:, 15:16], 2.0, None, A.mult, None, "wn", "wn2")
+    TC(T.c15[:, :], T.jpa[:, 15:16], "jpa", "c15")
+    MS(T.ordr[:, 0:16], -160.0 * S96, "or0")
+    MS(T.ol[:, 0:1], 0, "ol0")
+    TS(T.ul[:, :], T.iotac[:, 0:128:16], 160.0, None, A.add, None, "iotac", "ul")
+    MS(T.minus[:, :], -1.0, "minus", 2 * C)
+    MS(T.cb[:, 0:1], 160.0, "cb0")
+    for b in range(4):
+        QZ(T.eq[:, 128 * b:128 * b + 128], T.es[:, 128 * b:128 * b + 128], T.ef[:, 3 - b:515 - b], "ef", "eq%d" % b, 128)
 
     RK = {m: T.rk[:, C * i:C * i + C] for i, m in enumerate(POW)}
-    LK = {m: T.lk[:, 20 * i:20 * i + 20] for i, m in enumerate([1, 4, 16])}
-    OLALL = "ol0 ol1 ol2 ol3 ol4 ol5"
+    OL, OR = keys("ol", 0, C, 64), keys("or", 0, C, 64)
+    TC(T.lk[:, 0:20], T.nxi[:, :], "nxi", "lk0")
+    send(partner[0], [(T.gl[:, :], T.lk[:, 0:20])], "r_nx", "lk0", "gl", 700)
+    for i, m in enumerate(POW):
+        win, wk, l, c = (T.iotaT[:, :], "iotaT", 0, SPLIT[i]) if i == 0 else (RK[m // 2], "rk%da rk%db" % (i - 1, i - 1), i - 1, SPLIT[i])
+        if l: listed(T.lk[:, 20 * l:20 * l + 20], "lk%d" % l, *weigh(win, wk))
+        if c: GC("v", T.rk[:, C * i:C * i + 16 * c], win.indirect(T.lk[:, 20 * l:20 * l + c]), wk + " lk%d" % l, "rk%da" % i, 16 * c)
+        GC("a", T.rk[:, C * i + 16 * c:C * i + C], win.indirect(T.lk[:, 20 * l + c:20 * l + 20]), wk + " lk%d" % l, "rk%db" % i if c else "rk%da rk%db" % (i, i), C - 16 * c)
+    for at in POW + [128, 192, 256]:
+        m = min(at, 64)
+        i, n, lo, k = POW.index(m), max(m, 16), at // 16 * 16, at // 64
+        src = (at - m) // 16
+        GC("a", T.ordr[:, at:at + n], RK[m].indirect(T.ol[:, src:src + n // 16]), "rk%da rk%db ol%d" % (i, i, src // 4), "or%d" % k, n)
+        SCAN(T.wo[:, lo:lo + n], T.dR[:, 0:n], T.ordr[:, lo:lo + n], 0.0, A.mult, A.add, "dR or%d" % k, "wo%d" % k, n)
+        listed(T.ol[:, lo // 16:(lo + n) // 16], "ol%d" % k, T.wo[:, lo + 15:lo + n:16], "wo%d" % k)
+    for i in range(5):
+        TC(T.hr[:, :].indirect(T.lk[:, 4 * i:4 * i + 4]), T.iotaT[:, 64 * i:64 * i + 64], "lk0 iotaT", "hr", picked(64, SCATTER))
+    listed(T.inv[:, :], "inv", *weigh(T.hr[:, :], "hr"))
+    send(partner[0], [(T.hl[:, :], T.inv[:, :])], "r_h", "inv gone_r_nx", "hl", 80)
 
-    def times(m, by):
-        AC(RK[m + by], RK[m].indirect(LK[by]), "rk%d lk%d" % (m, by), "rk%d" % (m + by))
+    QZ(T.uq[:, :], T.us[:, :], T.ut[:, :], "ut", "uq", 128)
+    TC(T.uw[:, :].bitcast(dt.uint32), T.uq[:, :].bitcast(dt.uint32).indirect(T.ul[:, :]), "uq ul", "uwc", picked(128))
+    op("a", lambda: sc.activation(T.uws[:, :], T.us[:, :].indirect(T.ul[:, :]), ACT.Copy), "uq ul", "uws", picked(128))
 
-    def listed(m):
-        weigh(RK[m], "rk%d" % m, to_wlist(LK[m], "lk%d" % m))
+    def xname(r): return T["xq%d" % r], T["xs%d" % r], "xq%d_0 xq%d_1" % (r, r)
 
-    def digit(l, d, m, lst, k):
-        TT(T.og[:, 16 * d - 16:16 * d], RK[m].indirect(lst), T["low%d" % l][:, 16 * d - 16:16 * d], A.mult, "rk%d low%d " % (m, l) + k, "og%d" % d)
+    def quant(r, h):
+        q, s, xk = xname(r)
+        lo, hi = PIECES[h]
+        QZ(q[:, lo:hi], s[:, lo:hi], (T.xt if r else T.xin)[:, 4 * lo:4 * hi], keys("xt%d" % h, 0, 4, 1), "xq%d_%d" % (r, h), hi - lo)
 
-    def digits(l, out, wr):
-        op("v", lambda: ve.tensor_reduce(T.ov[:, l:l + 1], T.og[:, :], AxisListType.X, A.add), "og1 og2 og3", "ov%d" % l)
-        gap()
-        TS(T.of[:, l + 1:l + 2], T.of[:, l:l + 1], T.nb[:, l:l + 1], T.ov[:, l:l + 1], A.mult, A.add, "of%d nb%d ov%d" % (l, l, l), "of%d" % (l + 1))
-        gap()
-        TS(out, T.of[:, l + 1:l + 2], P96, 160.0, A.mult, A.add, "of%d" % (l + 1), wr)
-
-    def xname(r): return T["xq%d" % r], T["xs%d" % r], "xq%d" % r
-
-    def quant_x(r):
-        q, s, k = xname(r)
-        t, tk = (T.xin, "xin") if r == 0 else (T.xt, "xt0 xt1 xt2 xt3")
-        QZ(q[:, :], s[:, :], t[:, :], tk, k)
-
-    def quant_e(b):
-        QZ(T.eq[:, 128 * b:128 * b + 128], T.es[:, 128 * b:128 * b + 128], T.ef[:, 3 - b:515 - b], "ef", "eq%d" % b)
-
-    def spread(r, q, s, k, banks):
+    def spread(q, s, k, banks, out, wr):
         for b in range(4):
-            MM(T["ps%d" % banks[b]][:, 0:C], T.eq[:, 128 * b:128 * b + 128], T.es[:, 128 * b:128 * b + 128], q[:, :], s[:, :], "eq%d " % b + k, "ps%d" % banks[b])
-
-    NEAR, FAR = [1, 2, 3, 4], [5, 6, 7, 0]
-
-    def start(r):
-        q, s, k = xname(r)
-        send(partner[r], [(T["rq%d" % r][:, :].bitcast(dt.uint8), q[:, :].bitcast(dt.uint8)), (T["rs%d" % r][:, :], s[:, :])], "r_x%d" % r, k)
-        landed("r_x%d" % r, 2 * NE, "rq%d" % r)
-
-    def scores(r):
-        q, s, k = xname(r)
-        for p in (0, 7):
-            MM(T["ps%d" % p][:, 0:C], T.uw[:, :], T.uws[:, :], q[:, :], s[:, :], "uw " + k, "ps%d" % p)
-
-    def unpack(b):
-        AC(PLN(T.tb, b), T["ps%d" % NEAR[b]][:, 0:C], "ps%d" % NEAR[b], "tb%d" % b, 0.5)
-
-    def unpack_far(r):
-        q, s, k = T["rq%d" % r], T["rs%d" % r], "rq%d" % r
-        spread(r, q, s, k, FAR)
-        for b in range(4):
-            AC(PLN(T.tp, b), T["ps%d" % FAR[b]][:, 0:C], "ps%d" % FAR[b], "tp%d" % b, 0.5)
+            ps = "ps%d" % banks[b]
+            MM(T[ps][:, 0:C], T.eq[:, 128 * b:128 * b + 128], T.es[:, 128 * b:128 * b + 128], q[:, :], s[:, :], "eq%d " % b + k, ps, C)
+            AC(PLN(out, b), T[ps][:, 0:C], ps, wr + str(b), plain(C), 0.5)
 
     def guests(r):
         if r == 0: return T.gl[:, :], T.hl[:, :], "gl", "hl"
         return T["glab%d" % r][:, 0:20], T["glab%d" % r][:, 20:40], "glab%d" % r, "glab%d" % r
 
-    def f_u(r):
-        TS(T.uu[:, :], T.ps0[:, 0:C], 0.0, None, A.is_gt, None, "ps0", "uu")
-        op("a", lambda: sc.activation(T.sg[:, :], T.ps7[:, 0:C], ACT.Sign), "ps7", "sg")
+    def places():
+        v, k = weigh(T.posr[:, :], "posr")
+        TS(T.pos2[:, :], v, T.wn2[:, 0:1], 320.0, A.mult, A.add, k + " wn2", "pos2")
+        return v, k
 
-    def f_sv(r):
-        gL, hL, gk, hk = guests(r)
-        TT(T.svc[:, :], T.uu[:, :].indirect(hL), T.sg[:, :], A.is_ge, "uu sg " + hk, "svc")
-
-    def f_lv():
-        SCAN(T.lvs[:, :], T.d3[:, :], T.svc[:, :], 0.0, A.mult, A.add, "svc d3", "lvs")
-        gap()
-        TS(T.lv[:, :], T.lvs[:, 15:C:16], T.thr[:, 0:1], None, A.is_lt, None, "lvs thr", "lv")
-
-    TC(LK[1], T.nxi[:, :], "nxi", "lk1")
-    AC(RK[1], T.iotac[:, :].indirect(LK[1]), "iotac lk1", "rk1", S96)
-    for d in range(1, 4):
-        TC(T.low0[:, 16 * d - 16 + d:16 * d:4], T.M[:, d:16:4], "M", "low0")
-        TC(T.low1[:, 16 * d - 16 + 4 * d:16 * d - 12 + 4 * d], T.M[:, 4 * d:4 * d + 4], "M", "low1")
-    op("v", lambda: ve.tensor_reduce(T.nb[:, 0:1], T.M[:, 0:16:4], AxisListType.X, A.add), "M", "nb0")
-    op("v", lambda: ve.tensor_reduce(T.nb[:, 1:2], T.M[:, 0:4], AxisListType.X, A.add), "M", "nb1")
-    times(1, 1); times(2, 1); times(3, 1)
-    AC(T.iotaT[:, :], T.iotac[:, :], "iotac", "iotaT", S96)
-    TS(T.dR[:, :], T.M[:, :], -16384.0, 16384.0, A.mult, A.add, "M", "dR")
-    TS(T.dI[:, :], T.M[:, 0:16], -2.0 ** -14, 2.0 ** -14, A.mult, A.add, "M", "dI")
-    TS(T.mP[:, :], T.M[:, 0:16], P96, None, A.mult, None, "M", "mP")
-    digit(0, 1, 1, T.ou[:, 0:1], "ou")
-    SCAN(T.wn[:, :], T.dI[:, :], T.mP[:, :], 0.0, A.mult, A.add, "dI mP", "wn")
-    MS(T.cb[:, 0:1], -160.0, "cb0")
-    digit(0, 2, 2, T.ou[:, 0:1], "ou")
-    TS(T.wn2[:, :], T.wn[:, 15:16], 2.0, None, A.mult, None, "wn", "wn2")
-    TS(T.d3[:, :], T.M[:, :], -3.0, 3.0, A.mult, A.add, "M", "d3")
-    quant_e(0); quant_e(1)
-    digit(0, 3, 3, T.ou[:, 0:1], "ou")
-    quant_e(2); quant_e(3)
-    fillers += [lambda: TC(T.ul[:, :], T.c16[:, :], "c16", "ul"),
-                lambda: MS(T.fi[:, 0:1], 0.0, "fi0")]
-    listed(4)
-    times(4, 4); times(8, 4); times(12, 4)
-    fillers += [lambda: SCAN(T.th3[:, :], T.d3[:, 0:16], T.M[:, 0:16], 0.0, A.mult, A.add, "d3 M", "th3"),
-                lambda: MS(T.fi[:, 1287:1288], 1.0, "fi1")]
-    digits(0, T.ou1[:, 0:1], "ou1")
-    TS(T.thr[:, :], T.th3[:, 15:16], 0.75, None, A.mult, None, "th3", "thr")
-    digit(1, 1, 4, T.ou1[:, 0:1], "ou1")
-    quant_x(0)
-    start(0)
-    digit(1, 2, 8, T.ou1[:, 0:1], "ou1")
-    QZ(T.uq[:, :], T.us[:, :], T.ut[:, :], "ut", "uq")
-    TC(T.uw[:, :].bitcast(dt.uint32), T.uq[:, :].bitcast(dt.uint32).indirect(T.ul[:, :]), "uq ul", "uwc")
-    digit(1, 3, 12, T.ou1[:, 0:1], "ou1")
-    op("a", lambda: sc.activation(T.uws[:, :], T.us[:, :].indirect(T.ul[:, :]), ACT.Copy), "uq ul uwc", "uw")
-    listed(16)
-    scores(0)
-    times(16, 16); times(32, 16); times(48, 16)
-    fillers += [lambda: TC(T.gl[:, :], T.rnx[:, :], "rnx", "gl")]
-    digits(1, T.ol[:, 0:1], "ol0")
-    spread(0, T.xq0, T.xs0, "xq0", NEAR)
-    S20 = 2.0 ** -20
-    AC(T.jS[:, :], T.jf[:, :], "jf", "jS", S20)
-    ID(T.KE[:, :], T.jf[:, :], 641 * 512 * S20, 1024 * S20, "jf", "KE")
-    op("v", lambda: ve.tensor_copy(T.hr[:, :].indirect(T.gl[:, :]), T.iotaT[:, :]), "gl iotaT", "hr")
-    conv([(RK[16 * d], T.ol[:, 0:1], "rk%d ol0" % (16 * d), 16) for d in range(1, 4)], to_list(T.ol[:, 1:4], "ol1"))
-    for i in range(4):
-        if i == 0: fillers += [lambda: f_u(0)]
-        if i == 1: weigh(T.hr[:, :], "hr", to_wlist(T.hl[:, :], "hl"))
-        if i == 1:
-            ID(T.KO[:, :], T.jf[:, :], 642 * 512 * S20, 1024 * S20, "jf", "KO")
-            AC(T.M20[:, :], T.M[:, :], "M", "M20", 2.0 ** 20)
-            AC(T.rst2[:, 0:C], T.rst[:, :], "rst", "rst2a")
-        if i == 2: fillers += [lambda: f_sv(0)]
-        if i == 3: fillers += [lambda: f_lv()]
-        conv([(RK[64], T.ol[:, 4 * i:4 * i + 4], "rk64 " + ("ol0 ol1" if i == 0 else "ol%d" % (i + 1)), 64)], to_list(T.ol[:, 4 * i + 4:4 * i + 8], "ol%d" % (i + 2)))
-    gap(len(fillers))
-
-    def slots(r):
-        gL, hL, gk, hk = guests(r)
-        AC(T.gsv[:, :], T.svc[:, :].indirect(gL), "svc " + gk, "gsv")
-        (TC if r else AC)(T.vf[:, 0:2 * C:2], T.svc[:, :].indirect(T.ol[:, :]), "svc " + OLALL, "vfa")
-        ID(T.vf[:, 1:2 * C:2], T.gsv[:, :].indirect(T.ol[:, :]), 1.0, -1.0, "gsv " + OLALL, "vfb")
-
-    def holes():
-        ID(T.nvf[:, :], T.vf[:, :], 1.0, -1.0, "vfa vfb", "nvf")
-
-    def cap_even(): TT(T.cap[:, 0:2 * C:2], T.jS[:, :].indirect(T.ol[:, :]), T.KE[:, :], A.add, "jS KE " + OLALL, "capa")
-
-    def cap_odd(): TT(T.cap[:, 1:2 * C:2], T.gS[:, :].indirect(T.ol[:, :]), T.KO[:, :], A.add, "gS KO " + OLALL, "capb")
-
-    def guest_cols(r):
-        gL, hL, gk, hk = guests(r)
-        AC(T.gS[:, :], T.jS[:, :].indirect(gL), "jS " + gk, "gS")
-
-    def host_at(r):
-        gL, hL, gk, hk = guests(r)
-        AC(T.phr[:, :], T.posr[:, :].indirect(hL), "posr " + hk, "phr")
-
-    def host_place():
-
-        def fin(v, k):
-            TS(T.ph2[:, :], v, T.wn2[:, 0:1], 321.0, A.mult, A.add, k + " wn2", "ph2")
-            gap()
-            TT(T.dq[:, :], T.ph2[:, :], T.pos2[:, :], A.subtract, "ph2 pos2", "dq")
-        weigh(T.phr[:, :], "phr", fin)
-
-    slots(0)
-    op("v", lambda: ve.tensor_copy(T.posr[:, :].indirect(T.ol[:, :]), T.iotaT[:, :]), "iotaT " + OLALL, "posr")
-    host_at(0)
-    guest_cols(0)
-    holes()
-    AC(T.rst2[:, C:], T.rst[:, :], "rst", "rst2b")
-    for b in range(4): unpack(b)
-    fillers += [cap_even]
-    weigh(T.posr[:, :], "posr", lambda v, k: TS(T.pos2[:, :], v, T.wn2[:, 0:1], 320.0, A.mult, A.add, k + " wn2", "pos2"))
-    fillers += [cap_odd]
-    host_place()
-
+    quant(0, 0)
+    quant(0, 1)
+    DA, DB, NA, NB = (keys(k, 0, len(FIRST), 1) for k in ("da", "db", "na", "nb"))
     for r in range(3):
-        lab, rlab, lk, rk = T["lab%d" % r], T["rlab%d" % r], "lab%d" % r, "rlab%d" % r
+        q, s, xk = xname(r)
+        lab, rlab, rk = T["lab%d" % r], T["rlab%d" % r], "rlab%d" % r
+        la, lb = "la%d" % r, "lb%d" % r
+        gL, hL, gk, hk = guests(r)
         last = r == 2
-        if r:
-            quant_x(r)
-            start(r)
-            scores(r)
-            q, s, k = xname(r)
-            spread(r, q, s, k, NEAR)
-            cap_even()
-            f_u(r)
-            unpack(0)
-            f_sv(r)
-            slots(r)
-            holes()
-            fillers += [cap_odd]
-            f_lv()
-            gap(len(fillers))
-            unpack(1); unpack(2); unpack(3)
-        unpack_far(r)
-        TT(T.t1[:, :], T.lv[:, :], T.dq[:, :], A.mult, "lv dq", "t1")
-        TT(T.t2[:, :], T.t1[:, :], T.pos2[:, :], A.add, "t1 pos2", "t2")
-        SCAN(T.fi[:, 1:641], T.vf[:, :], T.cap[:, :], 0.0, A.max, A.min, "vfa vfb capa capb", "fif")
+        for h, (lo, hi) in enumerate(PIECES):
+            n, k = hi - lo, "xq%d_%d" % (r, h)
+            MM(T["ps%d" % h][:, 0:n], T.uw[:, :], T.uws[:, :], q[:, lo:hi], s[:, lo:hi], "uwc uws " + k, "ps%d" % h, n)
+            AF(ACT.Sign, T.w2[:, lo:hi], T["ps%d" % h][:, 0:n], -2.0 ** -100, 1.0, "ps%d" % h, "w2%d" % h, plain(n))
+            if h == 0 or r == 0:
+                AF(ACT.Sign, T.w1[:, lo:hi], T["ps%d" % h][:, 0:n], -2.0 ** -100, 1.0, "ps%d" % h, "w1%d" % h, plain(n))
+            else:
+                MM(T.ps2[:, 0:n], T.uw[:, :], T.uws[:, :], q[:, lo:hi], s[:, lo:hi], "uwc uws " + k, "ps2", n)
+                TS(T.w1[:, lo:hi], T.ps2[:, 0:n], 0.0, None, A.is_gt, None, "ps2", "w11", cost(n, 1))
+        send(partner[r], [(T["rq%d" % r][:, :].bitcast(dt.uint8), q[:, :].bitcast(dt.uint8)), (T["rs%d" % r][:, :], s[:, :])], "r_x%d" % r, xk, "rq%d" % r, 1600)
+        TT(T.lvc[:, :], T.w1[:, :].indirect(hL), T.w2[:, :], A.is_lt, "w10 w11 w20 w21 " + hk, "lvc", picked(C))
+        AF(ACT.Identity, T.svc[:, :], T.lvc[:, :], 1.0, -1.0, "lvc", "svc", plain(C))
+        if r == 0:
+            AC(T.gR[:, :], T.iotaT[:, :].indirect(gL), "iotaT " + gk, "gR", picked(C))
+            TT(T.lcg[:, :], T.lvc[:, :].indirect(gL), T.gR[:, :], A.mult, "lvc gR " + gk, "lcg", picked(C))
+            SCAN(T.lvs[:, :], T.dX[:, :], T.lvc[:, :], 0.0, A.add, A.max, "dX lvc", "lvs", C)
+            TS(T.lv[:, :], T.lvs[:, 15:C:16], T.c15[:, 0:1], None, A.subtract, None, "lvs c15", "lv")
+            TS(T.sv[:, :], T.lv[:, :], -1.0, 1.0, A.mult, A.add, "lv", "sv")
+            TS(T.lw[:, :], T.lv[:, :], T.wn2[:, 0:1], None, A.mult, None, "lv wn2", "lw")
+            TS(T.l3[:, :], T.lv[:, :], 321.0, None, A.mult, None, "lv", "l3")
+            for i in range(5):
+                TC(T.posr[:, :].indirect(T.ol[:, 4 * i:4 * i + 4]), T.iotaT[:, 64 * i:64 * i + 64], "iotaT ol%d" % i, "posr", picked(64, SCATTER))
+            AC(T.phr[:, :], T.posr[:, :].indirect(hL), "posr " + hk, "phr", picked(C))
+            for i, (lo, hi) in enumerate(FIRST):
+                o, ok, n = T.ol[:, lo // 16:hi // 16], keys("ol", lo, hi, 64), hi - lo
+                TT(T.d1[:, 2 * lo:2 * hi:2], T.svc[:, :].indirect(o), T.ordr[:, lo:hi], A.mult, "svc %s %s" % (ok, keys("or", lo, hi, 64)), "da%d" % i, picked(n))
+                AC(T.d1[:, 2 * lo + 1:2 * hi:2], T.lcg[:, :].indirect(o), "lcg " + ok, "db%d" % i, picked(n))
+                TS(T.nv[:, 2 * lo:2 * hi], T.d1[:, 2 * lo:2 * hi], 0.0, None, A.is_equal, None, "da%d db%d" % (i, i), "na%d nb%d" % (i, i), cost(n, 1))
+            places()
+            TT(T.t0[:, :], T.pos2[:, :], T.sv[:, :], A.mult, "pos2 sv", "t0")
+            TT(T.kq[:, :], T.t0[:, :], T.l3[:, :], A.add, "t0 l3", "kq")
+            v, k = weigh(T.phr[:, :], "phr")
+            TT(T.t1[:, :], v, T.lw[:, :], A.mult, k + " lw", "t1")
+        else:
+            TT(T.d1[:, 1:2 * C:2], T.lvc[:, :].indirect(T.go[:, :]), T.goR[:, :], A.mult, "lvc go goR", DB, picked(C))
+            SCAN(T.lvs[:, :], T.dX[:, :], T.lvc[:, :], 0.0, A.add, A.max, "dX lvc", "lvs", C)
+            TT(T.d1[:, 0:2 * C:2], T.svc[:, :].indirect(T.ol[:, :]), T.ordr[:, :], A.mult, "svc " + OL + " " + OR, DA, picked(C))
+            AC(T.nv[:, 0:2 * C:2], T.lvc[:, :].indirect(T.ol[:, :]), "lvc " + OL, NA, picked(C))
+            AF(ACT.Identity, T.nv[:, 1:2 * C:2], T.lvc[:, :].indirect(T.go[:, :]), 1.0, -1.0, "lvc go", NB, picked(C))
+            TT(T.t1[:, :], T.lvs[:, 15:C:16], T.dq[:, :], A.mult, "lvs dq", "t1")
+        TT(T.t2[:, :], T.t1[:, :], T.kq[:, :], A.add, "t1 kq", "t2")
         TC(T.ql[:, :], T.t2[:, :], "t2", "ql")
-        SCAN(T.fi[:, 1286:646:-1], T.nvf[:, ::-1], T.cap[:, ::-1], 1.0, A.min, A.max, "nvf capa capb", "fib")
-        TT(T.xm[:, C:], T.fi[:, 0:640].indirect(T.ql[:, :]), T.M20[:, :], A.mult, "fif fi0 ql M20", "xmb")
-        TT(T.xm[:, 0:C], T.fi[:, 648:1288].indirect(T.ql[:, :]), T.M20[:, :], A.mult, "fib fi1 ql M20", "xma")
-        TS(T.wr[:, :], T.fi[:, 640:648:7], 2.0 ** 20, None, A.mult, None, "fif fib", "wr")
-        SCAN(T.xsc[:, :], T.rst2[:, :], T.xm[:, :], 0.0, A.mult, A.add, "rst2a rst2b xma xmb", "xsc")
-        TS(T.di[:, 0:20], T.xsc[:, 15:C:16], -327680.0, T.wr[:, 1:2], A.add, A.min, "xsc wr", "dia")
-        TS(T.di[:, 20:40], T.xsc[:, C + 15:2 * C:16], 327680.0, T.wr[:, 0:1], A.add, A.max, "xsc wr", "dib")
-        TS(T.da[:, :], T.di[:, :], 511, None, A.bitwise_and, None, "dia dib", "da")
-        TC(lab[:, :], T.da[:, :], "da", lk)
-        send(partner[r], [(rlab[:, :], lab[:, :])], "r_l%d" % r, lk)
-        landed("r_l%d" % r, NE, rk)
+        sl = " ".join([DA, DB, NA, NB])
+        SCAN(T.ff[:, 0:HEAD], T.nv[:, 2 * C - HEAD:], T.d1[:, 2 * C - HEAD:], 0.0, A.mult, A.add, sl, "ff0", HEAD)
+        SCAN(T.fb[:, 14 + 2 * C + HEAD:14 + 2 * C:-1], T.nv[:, HEAD - 1::-1], T.d1[:, HEAD - 1::-1], 0.0, A.mult, A.add, sl, "fb0", HEAD)
+        SCAN(T.ff[:, HEAD:], T.nv[:, :], T.d1[:, :], T.ff[:, HEAD - 1:HEAD], A.mult, A.add, sl + " ff0", "ff1", 2 * C)
+        SCAN(T.fb[:, 14 + 2 * C:14:-1], T.nv[:, ::-1], T.d1[:, ::-1], T.fb[:, 15 + 2 * C:16 + 2 * C], A.mult, A.add, sl + " fb0", "fb1", 2 * C)
+        GC("a", T.bR[:, :], T.ff[:, HEAD - 1:HEAD - 1 + 2 * C].indirect(T.ql[:, :]), "ff0 ff1 ql", "bR", C)
+        GC("v", T.aR[:, :], T.fb[:, 16:16 + 2 * C].indirect(T.ql[:, :]), "fb0 fb1 ql", "aR", C)
+        listed(lab[:, 20:40], lb, *weigh(T.bR[:, :], "bR"))
+        listed(lab[:, 0:20], la, *weigh(T.aR[:, :], "aR"))
+        send(partner[r], [(rlab[:, :], lab[:, :])], "r_l%d" % r, la + " " + lb, rk, 80)
+        spread(q, s, xk, [3, 4, 5, 6], T.tb, "tb")
+        spread(T["rq%d" % r], T["rs%d" % r], "rq%d" % r, [7, 0, 1, 2], T.tp, "tp")
         if not last:
             n = r + 1
-            send(partner[n], [(T["glab%d" % n][:, :], lab[:, :])], "r_g%d" % n, lk)
-            landed("r_g%d" % n, NE, "glab%d" % n)
-        a, b_, ra, rb = lab[:, 0:20], lab[:, 20:40], rlab[:, 0:20], rlab[:, 20:40]
-        def own_b(b): AC(PLN(T.gb, b), PLN(T.tb, b).indirect(b_), "tb%d " % b + lk, "gb%d" % b)
-
-        if not last:
-            SCAN(T.cb[:, 1:641], T.vf[:, :], T.zero[:, :], -160.0, A.add, A.add, "vfa vfb zero", "cb")
-            TS(T.posr[:, :], T.cb[:, 0:640].indirect(T.ql[:, :]), S96, None, A.mult, None, "cb cb0 ql", "posr")
-
-            def fin(v, k):
-                TS(T.pu[:, :], v, T.wn[:, 15:16], 160.0, A.mult, A.add, k + " wn", "pu")
-                TS(T.pos2[:, :], v, T.wn2[:, 0:1], 320.0, A.mult, A.add, k + " wn2", "pos2")
-            weigh(T.posr[:, :], "posr", fin)
-            op("v", lambda: ve.tensor_copy(T.ordr[:, :].indirect(T.pu[:, :]), T.iotaT[:, :]), "pu iotaT", "ordr")
-        for b in range(4): own_b(b)
-        if last:
-            QZ(T.vq[:, :], T.vs[:, :], T.vt[:, :], "vt", "vq")
-        AC(T.zb[:, 0:160], PLN(T.tp, 0).indirect(rlab[:, 20:30]), "tp0 " + rk, "zb0a")
-        TC(T.zb[:, 160:C], PLN(T.tp, 0).indirect(rlab[:, 30:40]), "tp0 " + rk, "zb0")
-        for b in range(1, 4):
-            AC(PLN(T.zb, b), PLN(T.tp, b).indirect(rb), "tp%d " % b + rk, "zb%d" % b)
-        for b in range(4):
-            TT(T.zt[:, b:4 * C:4], PLN(T.tp, b).indirect(ra), PLN(T.zb, b), A.add, "tp%d zb%d " % (b, b) + rk + (" zb0a" if b == 0 else ""), "zt%d" % b)
-        QZ(T.zq[:, :], T.zs[:, :], T.zt[:, :], "zt0 zt1 zt2 zt3", "zq")
-        for b in range(4):
-            MM(T["ps%d" % (b + 1)][:, 0:C], T.wq[:, 128 * b:128 * b + 128], T.wsb[:, 128 * b:128 * b + 128], T.zq[:, :], T.zs[:, :], "wq wsb zq", "ps%d" % (b + 1))
-        if not last:
-            host_at(r + 1)
-            weigh(T.ordr[:, :], "ordr", to_wlist(T.ol[:, :], OLALL))
-            host_place()
-        for b in range(4):
-            AC(PLN(T.hb, b), T["ps%d" % (b + 1)][:, 0:C], "ps%d" % (b + 1), "hb%d" % b, 2.0 ** -6)
-        for b in range(4):
-            TT(T.xt[:, b:4 * C:4], PLN(T.hb, b).indirect(a), PLN(T.gb, b), A.add, "hb%d gb%d " % (b, b) + lk, "xt%d" % b)
-        if not last:
-            guest_cols(r + 1)
+            send(partner[n], [(T["glab%d" % n][:, :], lab[:, :])], "r_g%d" % n, la + " " + lb + " gone_r_l%d" % r, "glab%d" % n, 400)
+            SCAN(T.cb[:, 1:2 * C + 1], T.nv[:, :], T.minus[:, :], 160.0, A.add, A.add, NA + " " + NB + " minus", "cb", 2 * C)
+            TS(T.posr[:, :], T.cb[:, 0:2 * C].indirect(T.ql[:, :]), -S96, None, A.mult, None, "cb cb0 ql", "posr", picked(C))
+            listed(T.pu[:, :], "pu", *places())
+            TC(T.ordr[:, :].indirect(T.pu[:, :]), T.iotaT[:, :], "pu iotaT", OR, picked(C, SCATTER))
+            listed(T.ol[:, :], OL, *weigh(T.ordr[:, :], OR))
         else:
-            AC(T.nrr[:, :], T.jf[:, :].indirect(a), "jf " + lk, "nrr")
+            QZ(T.vq[:, :], T.vs[:, :], T.vt[:, :], "vt", "vq", 128)
+            AF(ACT.Identity, T.nrr[:, :], T.aR[:, :], 160.0, P96, "aR", "nrr", plain(C))
             dma("s", T.nr[:, :], T.nrr[0:128:16, :], "d_out", "nrr", "nr")
+        for b in range(4):
+            GC("a", PLN(T.gb, b), PLN(T.tb, b).indirect(lab[:, 20:40]), "tb%d " % b + lb, "gb%d" % b, C)
+        for h, (lo, hi) in enumerate(PIECES):
+            n = hi - lo
+            for b in range(4):
+                GC("v" if (h, b) == (1, 0) else "a", PLN(T.zb, b, lo, hi), PLN(T.tp, b).indirect(rlab[:, 20 + lo // 16:20 + hi // 16]), "tp%d " % b + rk, "zb%d%d" % (h, b), n)
+                TT(T.zt[:, 4 * lo + b:4 * hi:4], PLN(T.tp, b).indirect(rlab[:, lo // 16:hi // 16]), PLN(T.zb, b, lo, hi), A.add, "tp%d zb%d%d " % (b, h, b) + rk, "zt%d%d" % (h, b), picked(n))
+            QZ(T.zq[:, lo:hi], T.zs[:, lo:hi], T.zt[:, 4 * lo:4 * hi], keys("zt%d" % h, 0, 4, 1), "zq%d" % h, n)
+        for b in range(4):
+            for h, (lo, hi) in enumerate(PIECES):
+                n, ps = hi - lo, "ps%d" % (4 * h + b)
+                MM(T[ps][:, 0:n], T.wq[:, 128 * b:128 * b + 128], T.wsb[:, 128 * b:128 * b + 128], T.zq[:, lo:hi], T.zs[:, lo:hi], "wq wsb zq%d" % h, ps, n)
+                AC(PLN(T.hb, b, lo, hi), T[ps][:, 0:n], ps, "hb%d%d" % (h, b), plain(n), 2.0 ** -6)
+        for h, (lo, hi) in enumerate(PIECES):
+            for b in range(4):
+                TT(T.xt[:, 4 * lo + b:4 * hi:4], PLN(T.hb, b).indirect(lab[:, lo // 16:hi // 16]), PLN(T.gb, b, lo, hi), A.add, "hb0%d hb1%d gb%d " % (b, b, b) + la, "xt%d%d" % (h, b), picked(hi - lo))
+            quant(r + 1, h)
+        if not last:
+            gL, hL, gk, hk = guests(r + 1)
+            AC(T.gR[:, :], T.iotaT[:, :].indirect(gL), "iotaT " + gk, "gR", picked(C))
+            AC(T.goR[:, :], T.gR[:, :].indirect(T.ol[:, :]), "gR " + OL, "goR", picked(C))
+            listed(T.go[:, :], "go", *weigh(T.goR[:, :], "goR"))
+            AC(T.phr[:, :], T.posr[:, :].indirect(hL), "posr " + hk, "phr", picked(C))
+            v, k = weigh(T.phr[:, :], "phr")
+            TS(T.ph2[:, :], v, T.wn2[:, 0:1], 321.0, A.mult, A.add, k + " wn2", "ph2")
+            TT(T.dq[:, :], T.ph2[:, :], T.pos2[:, :], A.subtract, "ph2 pos2", "dq")
+            TS(T.t0[:, :], T.dq[:, :], T.nc15[:, 0:1], None, A.mult, None, "dq nc15", "t0")
+            TT(T.kq[:, :], T.t0[:, :], T.pos2[:, :], A.add, "t0 pos2", "kq")
 
-    q, s, k = xname(3)
-    quant_x(3)
-    MM(T.ps0[:, 0:C], T.vq[:, :], T.vs[:, :], q[:, :], s[:, :], "vq " + k, "ps0")
-    dma("s", T.oc[:, :], q[:, :].bitcast(dt.uint8), "d_out", k, "oc")
+    q, s, xk = xname(3)
+    for h, (lo, hi) in enumerate(PIECES):
+        n, ps, k = hi - lo, "ps%d" % h, "xq3_%d" % h
+        MM(T[ps][:, 0:n], T.vq[:, :], T.vs[:, :], q[:, lo:hi], s[:, lo:hi], "vq " + k, ps, n)
+        if h: TC(T.yo[:, lo:hi], T[ps][:, 0:n], ps, "yo1", cost(n, 1))
+        else: AC(T.yo[:, lo:hi], T[ps][:, 0:n], ps, "yo0", plain(n))
+        dma("s", T.oc[:, 4 * lo:4 * hi], q[:, lo:hi].bitcast(dt.uint8), "d_out", k, "oc%d" % h, 100)
+        dma("s", T.y[:, lo:hi], T.yo[:, lo:hi], "d_out", "yo%d" % h, "y%d" % h, 100)
     for i in range(4):
-        dma("a" if i % 2 else "s", T.osc[4 * i:4 * i + 4, :], s[32 * i:32 * i + 4, :], "d_out", k, "osc%d" % i)
-    TC(T.yo[:, :], T.ps0[:, 0:C], "ps0", "yo")
-    dma("s", T.y[:, :], T.yo[:, :], "d_out", "yo", "y")
+        dma("a", T.osc[4 * i:4 * i + 4, :], s[32 * i:32 * i + 4, :], "d_out", xk, "osc%d" % i)
+
+    if not ORDER: ORDER.extend(in_order(calls))
+    count, token = {}, {}
+    clock = {q: {} for q in Q}
+
+    def need(q, name, val, snap):
+        if clock[q].get(name, 0) < val:
+            Q[q].wait_ge(T.sem[name], val)
+            for k, v in list(snap.items()) + [(name, val)]:
+                clock[q][k] = max(clock[q].get(k, 0), v)
+
+    for i in ORDER:
+        c = calls[i]
+        q, sem = c["q"], c["sem"]
+        count[sem] = count.get(sem, 0) + c["inc"]
+        if q is None:
+            token[i] = (sem, count[sem], {})
+            continue
+        best = {}
+        for d in c["deps"]:
+            t = token[d]
+            if t[0] != "sent" and (t[0] not in best or best[t[0]][1] < t[1]): best[t[0]] = t
+        for t in best.values(): need(q, *t)
+        done = c["fn"]()
+        if sem != "sent": done.then_inc(T.sem[sem], c["inc"])
+        token[i] = (sem, count[sem], dict(clock[q]))
     for name in SEMAPHORES:
-        if count.get(name): need("s", (name, count[name], {}))
+        if count.get(name): need("s", name, count[name], {})

@@ -3,10 +3,11 @@ from concourse.mybir import dt, AluOpType, ActivationFunctionType
 N, C, MASK = 8, 320, [4, 1, 2]
 BF, F4, I4, U2, CO, PL = "bfloat16", "float32", "int32", "uint16", "float8_e4m3fn_x4", "uint8"
 POW = [1, 2, 4, 8, 16, 32, 64]
-SPLIT = [8, 8, 8, 8, 8, 8, 8]
 PIECES = [(0, 192), (192, C)]
+HALVES = [(0, 160), (160, C)]
 FIRST = [(0, 256), (256, C)]
 HEAD = 337
+ZB, ZT, XT = [0], [3], [3]
 SCRATCH = {}
 
 
@@ -17,7 +18,7 @@ def _sb(dtype, **kw):
 
 _sb(I4, nxi=20, jp=16, jpa=16)
 _sb(BF, xin=4 * C, ut=512, vt=512, xt=4 * C, zt=4 * C, tb=4 * C, tp=4 * C, hb=4 * C, gb=4 * C, zb=4 * C,
-    ones=516, ef=516, minus=2 * C, iotac=C, iotaT=C, dR=C, dX=C, dR16=16, dX16=16, rk=len(POW) * C, ws_=8 * C, wo=C,
+    ones=516, ef=516, minus=2 * C, iotac=C, iotaT=C, dR=C, dX=C, dR16=16, rk=len(POW) * C, ws_=8 * C, wo=C,
     hr=C, gR=C, goR=C, posr=C, phr=C, ordr=C, w1=C, w2=C, lvc=C, svc=C, lcg=C, lvs=C, aR=C, bR=C,
     nv=2 * C, d1=2 * C, ff=HEAD + 2 * C, fb=16 + 2 * C + HEAD, cb=2 * C + 16)
 _sb(F4, dI=16, mP=16, wn=16, wn2=1, c15=1, nc15=1, lv=20, sv=20, lw=20, l3=20, pos2=20, ph2=20, dq=20, kq=20, t0=20, t1=20, t2=20, nrr=C, yo=C)
@@ -35,44 +36,68 @@ _sb(PL, zs=C, us=128, uws=128, vs=128, wsb=512, es=512)
 for _r in range(8):
     SCRATCH["ps%d" % _r] = ("psum", [128, 512], F4)
 SEMAPHORES = ["cv", "ct", "ca", "cg", "d_nx", "d_x", "d_u", "d_wc", "d_ws", "d_v", "d_out", "sent", "r_nx", "r_h"] + \
-    ["r_x%d" % r for r in range(3)] + ["r_l%d" % r for r in range(3)] + ["r_g%d" % r for r in (1, 2)]
+    ["r_%s%d" % (k, r) for k in "xl" for r in range(3)] + ["r_g%d" % r for r in (1, 2)]
 
-CYCLE, GATHER, SCATTER, WAIT, LOAD, CALL, FLIGHT, BYTE = 0.95e-3, 1.56, 3.8, 0.12, 1.8, 0.25, 2.6, 1.5e-3
-PASSES, ORDER = 6, []
+PACES = [(0.83e-3, 1.3e-3, 3.2e-3, 0.15, 2.4), (1.15e-3, 2.1e-3, 5.5e-3, 0.12, 2.8)]
+SLACK, REACH, PLAN, MEASURE = [0, 0] + [0.05 * 0.85 ** i for i in range(18)] + [0, 0], 8, [], []
 
 
-def in_order(calls):
+def planned(calls):
     n = len(calls)
-    ahead, after = [c["deps"] for c in calls], [[] for c in calls]
+    queue, deps, hold = [[w[0] for w in c["ways"]] for c in calls], [c["deps"] for c in calls], [c["hold"] for c in calls]
+    time = [[[w[2][0] + w[2][1] * p[0] + w[2][2] * p[1] + w[2][3] * p[2] for w in c["ways"]] for c in calls] for p in PACES]
+    after, way = [[] for c in calls], [0] * n
     for i in range(n):
-        for d in ahead[i]: after[d].append(i)
+        for d in deps[i]: after[d].append(i)
 
-    def place(order, before):
-        start, busy = {}, {}
-        for i in order:
-            c = calls[i]
-            lead = 0.0 if before is ahead else c["time"] - c["hold"]
-            t = max([0.0] + [start[d] + calls[d]["time"] + WAIT for d in before[i]])
-            if c["q"] is not None:
-                taken = busy.setdefault(c["q"], [])
-                for lo, hi in taken:
-                    if hi > t + lead + 1e-9 and lo < t + lead + c["hold"] - 1e-9: t = hi - lead
-                taken.append((t + lead, t + lead + c["hold"]))
-                taken.sort()
-            start[i] = t
-        return start
+    def run(order):
+        total = 0.0
+        for m in (1, 0):
+            wait, tm, free, seen, start, rows = PACES[m][3], time[m], dict.fromkeys("vatgs", 0.0), [0.0] * n, [0.0] * n, 0.0
+            for i in order:
+                w = way[i]
+                q = queue[i][w]
+                t = free[q] if q else 0.0
+                for d in deps[i]:
+                    if seen[d] > t: t = seen[d]
+                start[i] = t
+                if q:
+                    end = t + tm[i][w]
+                    free[q] = t + hold[i] if hold[i] else end
+                else:
+                    end = rows = max(t + PACES[m][4], rows) + tm[i][w]
+                seen[i] = end + wait
+            total += (max(seen) + 0.03 * sum(start) / n) / (1 + m)
+        return total, start
 
-    tail = [c["time"] for c in calls]
-    for i in range(n - 1, -1, -1):
-        for d in ahead[i]: tail[d] = max(tail[d], calls[d]["time"] + WAIT + tail[i])
-    best = None
-    for order in (list(range(n)), sorted(range(n), key=lambda i: -tail[i])):
-        for _ in range(PASSES):
-            start = place(order, ahead)
-            end = max(start[i] + calls[i]["time"] for i in range(n))
-            if best is None or end < best[0]: best = (end, sorted(range(n), key=lambda i: (start[i], i)))
-            back = place(sorted(range(n), key=lambda i: (-start[i] - calls[i]["time"], -i)), after)
-            order = sorted(range(n), key=lambda i: (-back[i] - calls[i]["time"], i))
+    order = list(range(n))
+    measure, start = run(order)
+    best = (measure, [(i, 0) for i in order])
+    for slack in SLACK:
+        for i in range(n):
+            if queue[i][0] in (None, "s"): continue
+            now, keep = order.index(i), way[i]
+            rest = order[:now] + order[now + 1:]
+            at = {k: p for p, k in enumerate(rest)}
+            lo = max([0] + [at[d] + 1 for d in deps[i]])
+            hi = min([n - 1] + [at[d] for d in after[i]])
+            found = None
+            for w, q in enumerate(queue[i]):
+                marks = [p for p in range(lo, hi) if queue[rest[p]][way[rest[p]]] == q] + [hi]
+                same = min(p for p in marks if p >= now) if w == keep else None
+                marks.sort(key=lambda p: abs(p - now))
+                for p in marks[:REACH]:
+                    if p == same: continue
+                    way[i] = w
+                    trial = rest[:p] + [i] + rest[p:]
+                    got, st = run(trial)
+                    if got < measure + slack and (found is None or got < found[0]): found = (got, st, trial, w)
+            way[i] = keep
+            if found:
+                measure, start, order, way[i] = found
+                order.sort(key=lambda k: start[k])
+                if measure < best[0]: best = (measure, [(k, way[k]) for k in order])
+    MEASURE.append(best[0])
     return best[1]
 
 
@@ -85,42 +110,48 @@ def rank_program(g, core, T, topo):
     Q = {"v": ve, "t": te, "a": sc, "g": g, "s": sy}
     calls, wrote, read = [], {}, {}
 
-    def op(q, fn, rd, wr, time, sem=None, inc=1, hold=None):
+    def op(ways, rd, wr, sem=None, inc=1, hold=None):
         rd, wr, i = rd.split(), wr.split(), len(calls)
         deps = [wrote[k] for k in rd]
         for k in wr: deps += read.get(k, []) + ([wrote[k]] if k in wrote else [])
-        calls.append({"q": q, "fn": fn, "deps": sorted(set(deps)), "time": time, "hold": time if hold is None else hold, "sem": sem or "c" + q, "inc": inc})
+        calls.append({"ways": ways, "deps": sorted(set(deps)), "hold": hold, "sem": sem, "inc": inc})
         for k in rd: read.setdefault(k, []).append(i)
         for k in wr: wrote[k], read[k] = i, []
 
     def dma(q, out, in_, sem, rd, wr, kb=0):
-        op(q, lambda: Q[q].dma_start(out, in_), rd, wr, LOAD + kb / 200, sem, 16, 0.05)
+        op([(q, lambda: Q[q].dma_start(out, in_), (1.75 + kb / 200, 0, 0, 0))], rd, wr, sem, 16, 0.05)
 
-    def send(dst, pieces, rsem, rd, wr, width):
+    def send(dst, pieces, rsem, rd, wr, rows):
         rid, pid = topo.addr(dst, core)
         mask, n = topo.mask(core, dst), len(topo.engines(core, dst))
 
         def fn():
             for out, in_ in pieces: g.remote_dma(out, in_, T.sem[rsem], T.sem.sent, pid, rid, mask)
-        op("g", fn, rd, "gone_" + rsem, CALL * len(pieces), "sent", n * len(pieces))
-        op(None, None, "gone_" + rsem, wr, FLIGHT + BYTE * width, rsem, n * len(pieces))
+        op([("g", fn, (0.25 * len(pieces) + (rsem == "r_nx"), 0, 0, 0))], rd, "gone_" + rsem, "sent", n * len(pieces))
+        op([(None, None, (rows, 0, 0, 0))], "gone_" + rsem, wr, rsem, n * len(pieces))
 
-    def cost(n, rate): return max(64, n * rate) * CYCLE
-    def picked(n, rate=GATHER): return 0.06 + n * rate * CYCLE
-    def keys(name, lo, hi, step): return " ".join(name + str(i) for i in range(lo // step, (hi - 1) // step + 1))
+    def cyc(n=0, fixed=0.0): return (fixed, max(64, n), 0, 0)
+    def picked(n, fixed=0.05): return (fixed, 0, n, 0)
+    def strewn(n): return (0.05, 0, 0, n)
+    def keys(name, lo, hi, step=1): return " ".join(name + str(i) for i in range(lo // step, (hi - 1) // step + 1))
 
-    TT = lambda out, a, b, o, rd, wr, t=cost(0, 0): op("v", lambda: ve.tensor_tensor(out, a, b, o), rd, wr, t)
-    TS = lambda out, a, s1, s2, o, o2, rd, wr, t=cost(0, 0): op("v", (lambda: ve.tensor_scalar(out, a, s1, s2, o, o2)) if o2 is not None else (lambda: ve.tensor_scalar(out, a, s1, None, o)), rd, wr, t)
-    TC = lambda out, a, rd, wr, t=cost(0, 0): op("v", lambda: ve.tensor_copy(out, a), rd, wr, t)
-    SCAN = lambda out, a, b, i, o, o2, rd, wr, n: op("v", lambda: ve.tensor_tensor_scan(out, a, b, i, o, o2), rd, wr, cost(n, 0.5))
-    MS = lambda ap, c, wr, n=0: op("v", lambda: ve.memset(ap, c), "", wr, cost(n, 0.5))
-    AC = lambda out, a, rd, wr, t, scale=1.0: op("a", lambda: sc.activation(out, a, ACT.Copy, scale=scale), rd, wr, t)
-    AF = lambda f, out, a, bias, scale, rd, wr, t: op("a", lambda: sc.activation(out, a, f, bias=bias, scale=scale), rd, wr, t)
-    QZ = lambda q, s, t, rd, wr, n: op("v", lambda: ve.quantize_mx(q, s, t), rd, wr, 0.014 + n * 1e-3)
-    MM = lambda ps, l, ls, m, ms, rd, wr, n: op("t", lambda: te.matmul_mx(ps, l, ls, m, ms, True, True), rd, wr, (n + 16) * 0.9e-3)
+    V = lambda fn, rd, wr, t: op([("v", fn, t)], rd, wr)
+    TT = lambda out, a, b, o, rd, wr, t=cyc(): V(lambda: ve.tensor_tensor(out, a, b, o), rd, wr, t)
+    TS = lambda out, a, s1, s2, o, o2, rd, wr, t=cyc(): V((lambda: ve.tensor_scalar(out, a, s1, s2, o, o2)) if o2 is not None else (lambda: ve.tensor_scalar(out, a, s1, None, o)), rd, wr, t)
+    TC = lambda out, a, rd, wr, t=cyc(): V(lambda: ve.tensor_copy(out, a), rd, wr, t)
+    SCAN = lambda out, a, b, i, o, o2, rd, wr, n: V(lambda: ve.tensor_tensor_scan(out, a, b, i, o, o2), rd, wr, cyc(n // 2))
+    MS = lambda ap, c, wr, n=0: V(lambda: ve.memset(ap, c), "", wr, cyc(n // 2))
+    QZ = lambda q, s, t, rd, wr, n: V(lambda: ve.quantize_mx(q, s, t), rd, wr, (0.012, n * 1.06, 0, 0))
+    MM = lambda ps, l, ls, m, ms, rd, wr, n: op([("t", lambda: te.matmul_mx(ps, l, ls, m, ms, True, True), ((n + 16) * 0.9e-3, 0, 0, 0))], rd, wr)
     PLN = lambda buf, b, lo=0, hi=C: buf[:, C * b + lo:C * b + hi]
-    plain = lambda n: 0.06 + n * CYCLE
-    GC = lambda q, out, a, rd, wr, n: AC(out, a, rd, wr, picked(n)) if q == "a" else TC(out, a, rd, wr, picked(n))
+
+    def either(out, a, scale, bias, rd, wr, ta, tv, qs="av"):
+        ways = {"a": (lambda: sc.activation(out, a, ACT.Identity if bias else ACT.Copy, bias=bias, scale=scale), ta),
+                "v": (lambda: ve.tensor_scalar(out, a, scale, bias, A.mult, A.add) if bias else ve.tensor_scalar(out, a, scale, None, A.mult) if scale != 1.0 else ve.tensor_copy(out, a), tv)}
+        op([(q,) + ways[q] for q in qs], rd, wr)
+
+    GC = lambda out, a, rd, wr, n, scale=1.0, bias=0.0, qs="av": either(out, a, scale, bias, rd, wr, picked(n, 0.065), picked(n), qs)
+    PC = lambda out, ps, n, wr, scale, qs="av": either(out, T[ps][:, 0:n], scale, 0.0, "", wr + " " + ps, cyc(n, 0.06), cyc(n), qs)
     S96, P96 = 2.0 ** -96, 2.0 ** 96
     partner = [T.cores[rank ^ m] for m in MASK]
     turn = [0]
@@ -134,23 +165,23 @@ def rank_program(g, core, T, topo):
 
     dma("s", T.nxi[:, :], T.nx[:, :], "d_nx", "", "nxi")
     dma("s", T.ut[:, :], T.u[:, :], "d_u", "", "ut", 131)
-    dma("s", T.xin[:, :], T.x[:, :], "d_x", "", "xt00 xt01 xt02 xt03 xt10 xt11 xt12 xt13", 460)
+    dma("s", T.xin[:, :], T.x[:, :], "d_x", "", keys("xt0", 0, 4) + " " + keys("xt1", 0, 4), 460)
     dma("s", T.wq[:, :].bitcast(dt.uint8), T.wc[:, :], "d_wc", "", "wq", 720)
     dma("s", T.wsb[:, :], T.ws[:, :], "d_ws", "", "wsb", 790)
     dma("s", T.vt[:, :], T.v[:, :], "d_v", "", "vt", 920)
 
     MS(T.ones[:, :], 1.0, "ones", 516)
-    op("g", lambda: g.iota(T.jp[:, :], [[1, 16]], 0, -1), "", "jp", 0.13 + cost(16, 2))
-    op("g", lambda: g.affine_select(T.ef[:, :], T.ones[:, :], [[-1, 516]], A.is_equal, 0.0, 3, 4), "ones", "ef", 0.17 + cost(516, 2))
+    op([("g", lambda: g.iota(T.jp[:, :], [[1, 16]], 0, -1), cyc(32, 0.13))], "", "jp")
+    op([("g", lambda: g.affine_select(T.ef[:, :], T.ones[:, :], [[-1, 516]], A.is_equal, 0.0, 3, 4), cyc(1032, 0.17))], "ones", "ef")
     SCAN(T.iotac[:, :], T.ones[:, 0:C], T.ones[:, 0:C], -161.0, A.mult, A.add, "ones", "iotac", C)
-    TS(T.iotaT[:, :], T.iotac[:, :], S96, None, A.mult, None, "iotac", "iotaT", cost(C, 0.5))
+    TS(T.iotaT[:, :], T.iotac[:, :], S96, None, A.mult, None, "iotac", "iotaT", cyc(C // 2))
     MS(T.iotaT[:, 160:161], S96 * 2.0 ** -20, "iotaT")
     TS(T.jpa[:, :], T.jp[:, :], 15, None, A.bitwise_and, None, "jp", "jpa")
     TS(T.dR16[:, :], T.jpa[:, :], 0.0, 16384.0, A.not_equal, A.mult, "jpa", "dR16")
     TS(T.nc15[:, :], T.jpa[:, 15:16], -1.0, None, A.mult, None, "jpa", "nc15")
     TS(T.k16[:, :], T.ones[:, 0:20], T.nc15[:, 0:1], 15.0, A.mult, A.add, "ones nc15", "k16")
-    GC("a", T.dR[:, :], T.dR16[:, :].indirect(T.k16[:, :]), "dR16 k16", "dR", C)
-    AF(ACT.Identity, T.dX[:, :], T.dR[:, :], -256.0, 257.0 / 16384.0, "dR", "dX", plain(C))
+    GC(T.dR[:, :], T.dR16[:, :].indirect(T.k16[:, :]), "dR16 k16", "dR", C)
+    either(T.dX[:, :], T.dR[:, :], 257.0 / 16384.0, -256.0, "dR", "dX", cyc(C, 0.06), cyc(C // 2))
     TS(T.dI[:, :], T.dR16[:, :], 2.0 ** -28, None, A.mult, None, "dR16", "dI")
     TS(T.mP[:, :], T.jpa[:, :], 0.0, P96, A.is_equal, A.mult, "jpa", "mP")
     SCAN(T.wn[:, :], T.dI[:, :], T.mP[:, :], 0.0, A.mult, A.add, "dI mP", "wn", 0)
@@ -161,46 +192,37 @@ def rank_program(g, core, T, topo):
     TS(T.ul[:, :], T.iotac[:, 0:128:16], 160.0, None, A.add, None, "iotac", "ul")
     MS(T.minus[:, :], -1.0, "minus", 2 * C)
     MS(T.cb[:, 0:1], 160.0, "cb0")
-    for b in range(4):
-        QZ(T.eq[:, 128 * b:128 * b + 128], T.es[:, 128 * b:128 * b + 128], T.ef[:, 3 - b:515 - b], "ef", "eq%d" % b, 128)
-
-    RK = {m: T.rk[:, C * i:C * i + C] for i, m in enumerate(POW)}
-    OL, OR = keys("ol", 0, C, 64), keys("or", 0, C, 64)
-    TC(T.lk[:, 0:20], T.nxi[:, :], "nxi", "lk0")
-    send(partner[0], [(T.gl[:, :], T.lk[:, 0:20])], "r_nx", "lk0", "gl", 700)
-    for i, m in enumerate(POW):
-        win, wk, l, c = (T.iotaT[:, :], "iotaT", 0, SPLIT[i]) if i == 0 else (RK[m // 2], "rk%da rk%db" % (i - 1, i - 1), i - 1, SPLIT[i])
-        if l: listed(T.lk[:, 20 * l:20 * l + 20], "lk%d" % l, *weigh(win, wk))
-        if c: GC("v", T.rk[:, C * i:C * i + 16 * c], win.indirect(T.lk[:, 20 * l:20 * l + c]), wk + " lk%d" % l, "rk%da" % i, 16 * c)
-        GC("a", T.rk[:, C * i + 16 * c:C * i + C], win.indirect(T.lk[:, 20 * l + c:20 * l + 20]), wk + " lk%d" % l, "rk%db" % i if c else "rk%da rk%db" % (i, i), C - 16 * c)
-    for at in POW + [128, 192, 256]:
-        m = min(at, 64)
-        i, n, lo, k = POW.index(m), max(m, 16), at // 16 * 16, at // 64
-        src = (at - m) // 16
-        GC("a", T.ordr[:, at:at + n], RK[m].indirect(T.ol[:, src:src + n // 16]), "rk%da rk%db ol%d" % (i, i, src // 4), "or%d" % k, n)
-        SCAN(T.wo[:, lo:lo + n], T.dR[:, 0:n], T.ordr[:, lo:lo + n], 0.0, A.mult, A.add, "dR or%d" % k, "wo%d" % k, n)
-        listed(T.ol[:, lo // 16:(lo + n) // 16], "ol%d" % k, T.wo[:, lo + 15:lo + n:16], "wo%d" % k)
-    for i in range(5):
-        TC(T.hr[:, :].indirect(T.lk[:, 4 * i:4 * i + 4]), T.iotaT[:, 64 * i:64 * i + 64], "lk0 iotaT", "hr", picked(64, SCATTER))
-    listed(T.inv[:, :], "inv", *weigh(T.hr[:, :], "hr"))
-    send(partner[0], [(T.hl[:, :], T.inv[:, :])], "r_h", "inv gone_r_nx", "hl", 80)
-
-    QZ(T.uq[:, :], T.us[:, :], T.ut[:, :], "ut", "uq", 128)
-    TC(T.uw[:, :].bitcast(dt.uint32), T.uq[:, :].bitcast(dt.uint32).indirect(T.ul[:, :]), "uq ul", "uwc", picked(128))
-    op("a", lambda: sc.activation(T.uws[:, :], T.us[:, :].indirect(T.ul[:, :]), ACT.Copy), "uq ul", "uws", picked(128))
 
     def xname(r): return T["xq%d" % r], T["xs%d" % r], "xq%d_0 xq%d_1" % (r, r)
 
     def quant(r, h):
         q, s, xk = xname(r)
         lo, hi = PIECES[h]
-        QZ(q[:, lo:hi], s[:, lo:hi], (T.xt if r else T.xin)[:, 4 * lo:4 * hi], keys("xt%d" % h, 0, 4, 1), "xq%d_%d" % (r, h), hi - lo)
+        QZ(q[:, lo:hi], s[:, lo:hi], (T.xt if r else T.xin)[:, 4 * lo:4 * hi], keys("xt%d" % h, 0, 4), "xq%d_%d" % (r, h), hi - lo)
 
-    def spread(q, s, k, banks, out, wr):
-        for b in range(4):
-            ps = "ps%d" % banks[b]
-            MM(T[ps][:, 0:C], T.eq[:, 128 * b:128 * b + 128], T.es[:, 128 * b:128 * b + 128], q[:, :], s[:, :], "eq%d " % b + k, ps, C)
-            AC(PLN(out, b), T[ps][:, 0:C], ps, wr + str(b), plain(C), 0.5)
+    def scores(r, h):
+        q, s, xk = xname(r)
+        lo, hi = PIECES[h]
+        n = hi - lo
+        for i, w in ((1, T.w2), (0, T.w1)):
+            ps = "ps%d" % (2 * h + i)
+            MM(T[ps][:, 0:n], T.uw[:, :], T.uws[:, :], q[:, lo:hi], s[:, lo:hi], "uwc uws xq%d_%d" % (r, h), ps, n)
+            ways = [("a", (lambda w=w, ps=ps: sc.activation(w[:, lo:hi], T[ps][:, 0:n], ACT.Sign, bias=-2.0 ** -100)), cyc(n, 0.06))]
+            if i == 0: ways.insert(1 - (h and r > 0), ("v", (lambda ps=ps: ve.tensor_scalar(T.w1[:, lo:hi], T[ps][:, 0:n], 0.0, None, A.is_gt)), cyc(n)))
+            op(ways, ps, "w%d%d" % (i + 1, h))
+
+    def give_x(r):
+        q, s, xk = xname(r)
+        send(partner[r], [(T["rq%d" % r][:, :].bitcast(dt.uint8), q[:, :].bitcast(dt.uint8)), (T["rs%d" % r][:, :], s[:, :])], "r_x%d" % r, xk, "rq%d" % r, 2.8)
+
+    def unpack(r, b, far, qs="av"):
+        q, s, k = (T["rq%d" % r], T["rs%d" % r], "rq%d" % r) if far else xname(r)
+        ps = "ps%d" % (b if far else 4 + b)
+        MM(T[ps][:, 0:C], T.eq[:, 128 * b:128 * b + 128], T.es[:, 128 * b:128 * b + 128], q[:, :], s[:, :], "eq%d " % b + k, ps, C)
+        PC(PLN(T.tp if far else T.tb, b), ps, C, ("tp" if far else "tb") + str(b), 0.5, qs)
+
+    def runs(split):
+        return [(lo, hi, [h]) for h, (lo, hi) in enumerate(PIECES)] if split else [(0, C, [0, 1])]
 
     def guests(r):
         if r == 0: return T.gl[:, :], T.hl[:, :], "gl", "hl"
@@ -208,125 +230,191 @@ def rank_program(g, core, T, topo):
 
     def places():
         v, k = weigh(T.posr[:, :], "posr")
-        TS(T.pos2[:, :], v, T.wn2[:, 0:1], 320.0, A.mult, A.add, k + " wn2", "pos2")
-        return v, k
+        return v, k, lambda: TS(T.pos2[:, :], v, T.wn2[:, 0:1], 320.0, A.mult, A.add, k + " wn2", "pos2")
 
-    quant(0, 0)
-    quant(0, 1)
-    DA, DB, NA, NB = (keys(k, 0, len(FIRST), 1) for k in ("da", "db", "na", "nb"))
-    for r in range(3):
-        q, s, xk = xname(r)
-        lab, rlab, rk = T["lab%d" % r], T["rlab%d" % r], "rlab%d" % r
-        la, lb = "la%d" % r, "lb%d" % r
+    def leavers(r):
         gL, hL, gk, hk = guests(r)
-        last = r == 2
-        for h, (lo, hi) in enumerate(PIECES):
-            n, k = hi - lo, "xq%d_%d" % (r, h)
-            MM(T["ps%d" % h][:, 0:n], T.uw[:, :], T.uws[:, :], q[:, lo:hi], s[:, lo:hi], "uwc uws " + k, "ps%d" % h, n)
-            AF(ACT.Sign, T.w2[:, lo:hi], T["ps%d" % h][:, 0:n], -2.0 ** -100, 1.0, "ps%d" % h, "w2%d" % h, plain(n))
-            if h == 0 or r == 0:
-                AF(ACT.Sign, T.w1[:, lo:hi], T["ps%d" % h][:, 0:n], -2.0 ** -100, 1.0, "ps%d" % h, "w1%d" % h, plain(n))
-            else:
-                MM(T.ps2[:, 0:n], T.uw[:, :], T.uws[:, :], q[:, lo:hi], s[:, lo:hi], "uwc uws " + k, "ps2", n)
-                TS(T.w1[:, lo:hi], T.ps2[:, 0:n], 0.0, None, A.is_gt, None, "ps2", "w11", cost(n, 1))
-        send(partner[r], [(T["rq%d" % r][:, :].bitcast(dt.uint8), q[:, :].bitcast(dt.uint8)), (T["rs%d" % r][:, :], s[:, :])], "r_x%d" % r, xk, "rq%d" % r, 1600)
         TT(T.lvc[:, :], T.w1[:, :].indirect(hL), T.w2[:, :], A.is_lt, "w10 w11 w20 w21 " + hk, "lvc", picked(C))
-        AF(ACT.Identity, T.svc[:, :], T.lvc[:, :], 1.0, -1.0, "lvc", "svc", plain(C))
+        either(T.svc[:, :], T.lvc[:, :], -1.0, 1.0, "lvc", "svc", cyc(C, 0.06), cyc(C // 2))
+
+    def flags_listed():
+        SCAN(T.lvs[:, :], T.dX[:, :], T.lvc[:, :], 0.0, A.add, A.max, "dX lvc", "lvs", C)
+
+    def quant_e(b):
+        QZ(T.eq[:, 128 * b:128 * b + 128], T.es[:, 128 * b:128 * b + 128], T.ef[:, 3 - b:515 - b], "ef", "eq%d" % b, 128)
+
+    def quant_u():
+        QZ(T.uq[:, :], T.us[:, :], T.ut[:, :], "ut", "uq", 128)
+
+    def pick_u():
+        TC(T.uw[:, :].bitcast(dt.uint32), T.uq[:, :].bitcast(dt.uint32).indirect(T.ul[:, :]), "uq ul", "uwc", picked(128))
+        op([("a", lambda: sc.activation(T.uws[:, :], T.us[:, :].indirect(T.ul[:, :]), ACT.Copy), picked(128, 0.065))], "uq ul", "uws")
+
+    def place_of(i):
+        TC(T.posr[:, :].indirect(T.ol[:, 4 * i:4 * i + 4]), T.iotaT[:, 64 * i:64 * i + 64], "iotaT ol%d" % i, "posr", strewn(64))
+
+    def guest_cols(r):
+        gL, hL, gk, hk = guests(r)
+        GC(T.gR[:, :], T.iotaT[:, :].indirect(gL), "iotaT " + gk, "gR", C)
+
+    def guest_leaves():
+        TT(T.lcg[:, :], T.lvc[:, :].indirect(T.gl[:, :]), T.gR[:, :], A.mult, "lvc gR gl", "lcg", picked(C))
+
+    def first_slots(i):
+        lo, hi = FIRST[i]
+        o, ok, n = T.ol[:, lo // 16:hi // 16], keys("ol", lo, hi, 64), hi - lo
+        GC(T.d1[:, 2 * lo + 1:2 * hi:2], T.lcg[:, :].indirect(o), "lcg " + ok, "db%d" % i, n)
+        GC(T.nv[:, 2 * lo:2 * hi:2], T.lvc[:, :].indirect(o), "lvc " + ok, "na%d" % i, n)
+        TT(T.d1[:, 2 * lo:2 * hi:2], T.svc[:, :].indirect(o), T.ordr[:, lo:hi], A.mult, "svc %s %s" % (ok, keys("or", lo, hi, 64)), "da%d" % i, picked(n))
+        TS(T.nv[:, 2 * lo + 1:2 * hi:2], T.d1[:, 2 * lo + 1:2 * hi:2], 0.0, None, A.is_equal, None, "db%d" % i, "nb%d" % i, cyc(n // 2))
+
+    def by_flag():
+        TS(T.lv[:, :], T.lvs[:, 15:C:16], T.c15[:, 0:1], None, A.subtract, None, "lvs c15", "lv")
+        TS(T.sv[:, :], T.lv[:, :], -1.0, 1.0, A.mult, A.add, "lv", "sv")
+        TS(T.lw[:, :], T.lv[:, :], T.wn2[:, 0:1], None, A.mult, None, "lv wn2", "lw")
+        TS(T.l3[:, :], T.lv[:, :], 321.0, None, A.mult, None, "lv", "l3")
+
+    RK = {m: T.rk[:, C * i:C * i + C] for i, m in enumerate(POW)}
+    OL, OR = keys("ol", 0, C, 64), keys("or", 0, C, 64)
+    quant_e(0)
+    quant_e(1)
+    TC(T.lk[:, 0:20], T.nxi[:, :], "nxi", "lk0")
+    send(partner[0], [(T.gl[:, :], T.lk[:, 0:20])], "r_nx", "lk0", "gl", 0.55)
+    TC(T.hr[:, :].indirect(T.lk[:, 0:20]), T.iotaT[:, :], "lk0 iotaT", "hr", strewn(C))
+    listed(T.inv[:, :], "inv", *weigh(T.hr[:, :], "hr"))
+    send(partner[0], [(T.hl[:, :], T.inv[:, :])], "r_h", "inv gone_r_nx", "hl", 0.55)
+    beside = {2: [quant_u, lambda: quant(0, 1)], 4: [pick_u], 8: [lambda: quant(0, 0), lambda: scores(0, 0), lambda: scores(0, 1), lambda: give_x(0)],
+              16: [lambda: quant_e(2), lambda: quant_e(3), lambda: guest_cols(0)], 32: [lambda: place_of(0)],
+              64: [lambda: leavers(0), lambda: unpack(0, 0, False)], 128: [guest_leaves, lambda: unpack(0, 1, False)],
+              192: [lambda: place_of(1), lambda: place_of(2), flags_listed, lambda: place_of(3), lambda: first_slots(0), by_flag], 256: [lambda: place_of(4)]}
+    for i, m in enumerate(POW):
+        win, wk, l = (T.iotaT[:, :], "iotaT", 0) if i == 0 else (RK[m // 2], keys("rk%d" % (i - 1), 0, 2), i - 1)
+        if l: listed(T.lk[:, 20 * l:20 * l + 20], "lk%d" % l, *weigh(win, wk))
+        for h, (lo, hi) in enumerate(HALVES if l else [(0, C)]):
+            GC(T.rk[:, C * i + lo:C * i + hi], win.indirect(T.lk[:, 20 * l + lo // 16:20 * l + hi // 16]), wk + " lk%d" % l, "rk%d%d" % (i, h) if l else keys("rk%d" % i, 0, 2), hi - lo, qs="av"[::1 - 2 * h])
+        for at in [m] if m < POW[-1] else range(m, C, m):
+            n, lo, k = max(m, 16), at // 16 * 16, at // 64
+            src = (at - m) // 16
+            GC(T.ordr[:, at:at + n], RK[m].indirect(T.ol[:, src:src + n // 16]), keys("rk%d" % i, 0, 2) + " ol%d" % (src // 4), "or%d" % k, n)
+            SCAN(T.wo[:, lo:lo + n], T.dR[:, 0:n], T.ordr[:, lo:lo + n], 0.0, A.mult, A.add, "dR or%d" % k, "wo%d" % k, n)
+            listed(T.ol[:, lo // 16:(lo + n) // 16], "ol%d" % k, T.wo[:, lo + 15:lo + n:16], "wo%d" % k)
+            for f in beside.get(at, []): f()
+
+    DA, DB, NA, NB = (keys(k, 0, len(FIRST)) for k in ("da", "db", "na", "nb"))
+    both = lambda k, b, hs: " ".join("%s%d%d" % (k, h, b) for h in hs)
+    for r in range(3):
+        lab, rlab, la, lb, rk = T["lab%d" % r], T["rlab%d" % r], "la%d" % r, "lb%d" % r, "rlab%d" % r
+        last = r == 2
         if r == 0:
-            AC(T.gR[:, :], T.iotaT[:, :].indirect(gL), "iotaT " + gk, "gR", picked(C))
-            TT(T.lcg[:, :], T.lvc[:, :].indirect(gL), T.gR[:, :], A.mult, "lvc gR " + gk, "lcg", picked(C))
-            SCAN(T.lvs[:, :], T.dX[:, :], T.lvc[:, :], 0.0, A.add, A.max, "dX lvc", "lvs", C)
-            TS(T.lv[:, :], T.lvs[:, 15:C:16], T.c15[:, 0:1], None, A.subtract, None, "lvs c15", "lv")
-            TS(T.sv[:, :], T.lv[:, :], -1.0, 1.0, A.mult, A.add, "lv", "sv")
-            TS(T.lw[:, :], T.lv[:, :], T.wn2[:, 0:1], None, A.mult, None, "lv wn2", "lw")
-            TS(T.l3[:, :], T.lv[:, :], 321.0, None, A.mult, None, "lv", "l3")
-            for i in range(5):
-                TC(T.posr[:, :].indirect(T.ol[:, 4 * i:4 * i + 4]), T.iotaT[:, 64 * i:64 * i + 64], "iotaT ol%d" % i, "posr", picked(64, SCATTER))
-            AC(T.phr[:, :], T.posr[:, :].indirect(hL), "posr " + hk, "phr", picked(C))
-            for i, (lo, hi) in enumerate(FIRST):
-                o, ok, n = T.ol[:, lo // 16:hi // 16], keys("ol", lo, hi, 64), hi - lo
-                TT(T.d1[:, 2 * lo:2 * hi:2], T.svc[:, :].indirect(o), T.ordr[:, lo:hi], A.mult, "svc %s %s" % (ok, keys("or", lo, hi, 64)), "da%d" % i, picked(n))
-                AC(T.d1[:, 2 * lo + 1:2 * hi:2], T.lcg[:, :].indirect(o), "lcg " + ok, "db%d" % i, picked(n))
-                TS(T.nv[:, 2 * lo:2 * hi], T.d1[:, 2 * lo:2 * hi], 0.0, None, A.is_equal, None, "da%d db%d" % (i, i), "na%d nb%d" % (i, i), cost(n, 1))
-            places()
+            first_slots(1)
+            for h, (lo, hi) in enumerate(HALVES):
+                GC(T.phr[:, lo:hi], T.posr[:, :].indirect(T.hl[:, lo // 16:hi // 16]), "posr hl", "phr%d" % h, hi - lo)
+            places()[2]()
+            v, k = weigh(T.phr[:, :], "phr0 phr1")
             TT(T.t0[:, :], T.pos2[:, :], T.sv[:, :], A.mult, "pos2 sv", "t0")
-            TT(T.kq[:, :], T.t0[:, :], T.l3[:, :], A.add, "t0 l3", "kq")
-            v, k = weigh(T.phr[:, :], "phr")
             TT(T.t1[:, :], v, T.lw[:, :], A.mult, k + " lw", "t1")
+            TT(T.kq[:, :], T.t0[:, :], T.l3[:, :], A.add, "t0 l3", "kq")
         else:
+            unpack(r, 0, False)
+            leavers(r)
             TT(T.d1[:, 1:2 * C:2], T.lvc[:, :].indirect(T.go[:, :]), T.goR[:, :], A.mult, "lvc go goR", DB, picked(C))
-            SCAN(T.lvs[:, :], T.dX[:, :], T.lvc[:, :], 0.0, A.add, A.max, "dX lvc", "lvs", C)
+            GC(T.nv[:, 0:2 * C:2], T.lvc[:, :].indirect(T.ol[:, :]), "lvc " + OL, NA, C)
             TT(T.d1[:, 0:2 * C:2], T.svc[:, :].indirect(T.ol[:, :]), T.ordr[:, :], A.mult, "svc " + OL + " " + OR, DA, picked(C))
-            AC(T.nv[:, 0:2 * C:2], T.lvc[:, :].indirect(T.ol[:, :]), "lvc " + OL, NA, picked(C))
-            AF(ACT.Identity, T.nv[:, 1:2 * C:2], T.lvc[:, :].indirect(T.go[:, :]), 1.0, -1.0, "lvc go", NB, picked(C))
-            TT(T.t1[:, :], T.lvs[:, 15:C:16], T.dq[:, :], A.mult, "lvs dq", "t1")
-        TT(T.t2[:, :], T.t1[:, :], T.kq[:, :], A.add, "t1 kq", "t2")
-        TC(T.ql[:, :], T.t2[:, :], "t2", "ql")
+            TS(T.nv[:, 1:2 * C:2], T.d1[:, 1:2 * C:2], 0.0, None, A.is_equal, None, DB, NB, cyc(C // 2))
+            flags_listed()
+            unpack(r, 1, False)
+        unpack(r, 2, False)
         sl = " ".join([DA, DB, NA, NB])
         SCAN(T.ff[:, 0:HEAD], T.nv[:, 2 * C - HEAD:], T.d1[:, 2 * C - HEAD:], 0.0, A.mult, A.add, sl, "ff0", HEAD)
-        SCAN(T.fb[:, 14 + 2 * C + HEAD:14 + 2 * C:-1], T.nv[:, HEAD - 1::-1], T.d1[:, HEAD - 1::-1], 0.0, A.mult, A.add, sl, "fb0", HEAD)
+        if r: TT(T.t1[:, :], T.lvs[:, 15:C:16], T.dq[:, :], A.mult, "lvs dq", "t1")
+        SCAN(T.fb[:, 15 + 2 * C + HEAD // 2:14 + 2 * C:-1], T.nv[:, HEAD - 1::-2], T.d1[:, HEAD - 1::-2], 0.0, A.mult, A.add, DA + " " + NA, "fb0", HEAD // 2 + 1)
+        TT(T.t2[:, :], T.t1[:, :], T.kq[:, :], A.add, "t1 kq", "t2")
         SCAN(T.ff[:, HEAD:], T.nv[:, :], T.d1[:, :], T.ff[:, HEAD - 1:HEAD], A.mult, A.add, sl + " ff0", "ff1", 2 * C)
+        TC(T.ql[:, :], T.t2[:, :], "t2", "ql")
         SCAN(T.fb[:, 14 + 2 * C:14:-1], T.nv[:, ::-1], T.d1[:, ::-1], T.fb[:, 15 + 2 * C:16 + 2 * C], A.mult, A.add, sl + " fb0", "fb1", 2 * C)
-        GC("a", T.bR[:, :], T.ff[:, HEAD - 1:HEAD - 1 + 2 * C].indirect(T.ql[:, :]), "ff0 ff1 ql", "bR", C)
-        GC("v", T.aR[:, :], T.fb[:, 16:16 + 2 * C].indirect(T.ql[:, :]), "fb0 fb1 ql", "aR", C)
-        listed(lab[:, 20:40], lb, *weigh(T.bR[:, :], "bR"))
-        listed(lab[:, 0:20], la, *weigh(T.aR[:, :], "aR"))
-        send(partner[r], [(rlab[:, :], lab[:, :])], "r_l%d" % r, la + " " + lb, rk, 80)
-        spread(q, s, xk, [3, 4, 5, 6], T.tb, "tb")
-        spread(T["rq%d" % r], T["rs%d" % r], "rq%d" % r, [7, 0, 1, 2], T.tp, "tp")
+        GC(T.bR[:, :], T.ff[:, HEAD - 1:HEAD - 1 + 2 * C].indirect(T.ql[:, :]), "ff0 ff1 ql", "bR", C)
+        for h, (lo, hi) in enumerate(PIECES):
+            GC(T.aR[:, lo:hi], T.fb[:, 16:16 + 2 * C].indirect(T.ql[:, lo // 16:hi // 16]), "fb0 fb1 ql", "aR%d" % h, hi - lo, qs="va"[::1 - 2 * h])
+        wb, wa = weigh(T.bR[:, :], "bR"), weigh(T.aR[:, :], "aR0 aR1")
+        listed(lab[:, 20:40], lb, *wb)
+        listed(lab[:, 0:20], la, *wa)
+        send(partner[r], [(rlab[:, :], lab[:, :])], "r_l%d" % r, la + " " + lb, rk, 0.6)
+        unpack(r, 3, False)
+
+        def own_b(b, qs="av"): GC(PLN(T.gb, b), PLN(T.tb, b).indirect(lab[:, 20:40]), "tb%d " % b + lb, "gb%d" % b, C, qs=qs)
         if not last:
             n = r + 1
-            send(partner[n], [(T["glab%d" % n][:, :], lab[:, :])], "r_g%d" % n, la + " " + lb + " gone_r_l%d" % r, "glab%d" % n, 400)
+            send(partner[n], [(T["glab%d" % n][:, :], lab[:, :])], "r_g%d" % n, la + " " + lb + " gone_r_l%d" % r, "glab%d" % n, 0.6)
             SCAN(T.cb[:, 1:2 * C + 1], T.nv[:, :], T.minus[:, :], 160.0, A.add, A.add, NA + " " + NB + " minus", "cb", 2 * C)
-            TS(T.posr[:, :], T.cb[:, 0:2 * C].indirect(T.ql[:, :]), -S96, None, A.mult, None, "cb cb0 ql", "posr", picked(C))
-            listed(T.pu[:, :], "pu", *places())
-            TC(T.ordr[:, :].indirect(T.pu[:, :]), T.iotaT[:, :], "pu iotaT", OR, picked(C, SCATTER))
+            GC(T.posr[:, :], T.cb[:, 0:2 * C].indirect(T.ql[:, :]), "cb cb0 ql", "posr", C, -S96, qs="va")
+            v, k, twice = places()
+            listed(T.pu[:, :], "pu", v, k)
+            twice()
+            TC(T.ordr[:, :].indirect(T.pu[:, :]), T.iotaT[:, :], "pu iotaT", OR, strewn(C))
             listed(T.ol[:, :], OL, *weigh(T.ordr[:, :], OR))
+            own_b(0); own_b(1)
+            for b in range(4): unpack(r, b, True, "va" if b == 3 else "av")
+            own_b(2); own_b(3)
         else:
             QZ(T.vq[:, :], T.vs[:, :], T.vt[:, :], "vt", "vq", 128)
-            AF(ACT.Identity, T.nrr[:, :], T.aR[:, :], 160.0, P96, "aR", "nrr", plain(C))
+            either(T.nrr[:, :], T.aR[:, :], P96, 160.0, "aR0 aR1", "nrr", cyc(C, 0.06), cyc(C))
             dma("s", T.nr[:, :], T.nrr[0:128:16, :], "d_out", "nrr", "nr")
+            for b in range(4): own_b(b, "va")
+            for b in range(4): unpack(r, b, True)
         for b in range(4):
-            GC("a", PLN(T.gb, b), PLN(T.tb, b).indirect(lab[:, 20:40]), "tb%d " % b + lb, "gb%d" % b, C)
-        for h, (lo, hi) in enumerate(PIECES):
-            n = hi - lo
-            for b in range(4):
-                GC("v" if (h, b) == (1, 0) else "a", PLN(T.zb, b, lo, hi), PLN(T.tp, b).indirect(rlab[:, 20 + lo // 16:20 + hi // 16]), "tp%d " % b + rk, "zb%d%d" % (h, b), n)
-                TT(T.zt[:, 4 * lo + b:4 * hi:4], PLN(T.tp, b).indirect(rlab[:, lo // 16:hi // 16]), PLN(T.zb, b, lo, hi), A.add, "tp%d zb%d%d " % (b, h, b) + rk, "zt%d%d" % (h, b), picked(n))
-            QZ(T.zq[:, lo:hi], T.zs[:, lo:hi], T.zt[:, 4 * lo:4 * hi], keys("zt%d" % h, 0, 4, 1), "zq%d" % h, n)
-        for b in range(4):
-            for h, (lo, hi) in enumerate(PIECES):
-                n, ps = hi - lo, "ps%d" % (4 * h + b)
-                MM(T[ps][:, 0:n], T.wq[:, 128 * b:128 * b + 128], T.wsb[:, 128 * b:128 * b + 128], T.zq[:, lo:hi], T.zs[:, lo:hi], "wq wsb zq%d" % h, ps, n)
-                AC(PLN(T.hb, b, lo, hi), T[ps][:, 0:n], ps, "hb%d%d" % (h, b), plain(n), 2.0 ** -6)
-        for h, (lo, hi) in enumerate(PIECES):
-            for b in range(4):
-                TT(T.xt[:, 4 * lo + b:4 * hi:4], PLN(T.hb, b).indirect(lab[:, lo // 16:hi // 16]), PLN(T.gb, b, lo, hi), A.add, "hb0%d hb1%d gb%d " % (b, b, b) + la, "xt%d%d" % (h, b), picked(hi - lo))
-            quant(r + 1, h)
+            for lo, hi, hs in runs(b in ZB):
+                GC(PLN(T.zb, b, lo, hi), PLN(T.tp, b).indirect(rlab[:, 20 + lo // 16:20 + hi // 16]), "tp%d " % b + rk, both("zb", b, hs), hi - lo, qs="va" if (b, hs) == (0, [0]) else "av")
         if not last:
             gL, hL, gk, hk = guests(r + 1)
-            AC(T.gR[:, :], T.iotaT[:, :].indirect(gL), "iotaT " + gk, "gR", picked(C))
-            AC(T.goR[:, :], T.gR[:, :].indirect(T.ol[:, :]), "gR " + OL, "goR", picked(C))
-            listed(T.go[:, :], "go", *weigh(T.goR[:, :], "goR"))
-            AC(T.phr[:, :], T.posr[:, :].indirect(hL), "posr " + hk, "phr", picked(C))
-            v, k = weigh(T.phr[:, :], "phr")
+            GC(T.phr[:, :], T.posr[:, :].indirect(hL), "posr " + hk, "phr0 phr1", C)
+            guest_cols(r + 1)
+        for h, (l0, h0) in enumerate(PIECES):
+            for b in range(4):
+                for lo, hi, hs in runs(b in ZT):
+                    if hs[0] == h: TT(T.zt[:, 4 * lo + b:4 * hi:4], PLN(T.tp, b).indirect(rlab[:, lo // 16:hi // 16]), PLN(T.zb, b, lo, hi), A.add, "tp%d %s " % (b, both("zb", b, hs)) + rk, both("zt", b, hs), picked(hi - lo))
+            QZ(T.zq[:, l0:h0], T.zs[:, l0:h0], T.zt[:, 4 * l0:4 * h0], keys("zt%d" % h, 0, 4), "zq%d" % h, h0 - l0)
+
+        def layer(h, b, qs="av"):
+            lo, hi = PIECES[h]
+            n, ps = hi - lo, "ps%d" % (4 * h + b)
+            MM(T[ps][:, 0:n], T.wq[:, 128 * b:128 * b + 128], T.wsb[:, 128 * b:128 * b + 128], T.zq[:, lo:hi], T.zs[:, lo:hi], "wq wsb zq%d" % h, ps, n)
+            PC(PLN(T.hb, b, lo, hi), ps, n, "hb%d%d" % (h, b), 2.0 ** -6, qs)
+        layer(0, 0); layer(0, 1)
+        if not last:
+            v, k = weigh(T.phr[:, :], "phr0 phr1")
             TS(T.ph2[:, :], v, T.wn2[:, 0:1], 321.0, A.mult, A.add, k + " wn2", "ph2")
+        layer(1, 0, "va"); layer(1, 1)
+        if not last:
             TT(T.dq[:, :], T.ph2[:, :], T.pos2[:, :], A.subtract, "ph2 pos2", "dq")
-            TS(T.t0[:, :], T.dq[:, :], T.nc15[:, 0:1], None, A.mult, None, "dq nc15", "t0")
-            TT(T.kq[:, :], T.t0[:, :], T.pos2[:, :], A.add, "t0 pos2", "kq")
+        for b in (2, 3): layer(0, b); layer(1, b)
+        if not last:
+            GC(T.goR[:, :], T.gR[:, :].indirect(T.ol[:, :]), "gR " + OL, "goR", C)
+        for h in range(2):
+            for b in range(4):
+                for lo, hi, hs in runs(b in XT):
+                    if hs[0] == h: TT(T.xt[:, 4 * lo + b:4 * hi:4], PLN(T.hb, b).indirect(lab[:, lo // 16:hi // 16]), PLN(T.gb, b, lo, hi), A.add, "hb0%d hb1%d gb%d " % (b, b, b) + la, both("xt", b, hs), picked(hi - lo))
+            quant(r + 1, h)
+            if not last:
+                if h:
+                    wg = weigh(T.goR[:, :], "goR")
+                    TS(T.t0[:, :], T.dq[:, :], T.nc15[:, 0:1], None, A.mult, None, "dq nc15", "t0")
+                    listed(T.go[:, :], "go", *wg)
+                    TT(T.kq[:, :], T.t0[:, :], T.pos2[:, :], A.add, "t0 pos2", "kq")
+                scores(r + 1, h)
+        if not last: give_x(r + 1)
 
     q, s, xk = xname(3)
     for h, (lo, hi) in enumerate(PIECES):
         n, ps, k = hi - lo, "ps%d" % h, "xq3_%d" % h
         MM(T[ps][:, 0:n], T.vq[:, :], T.vs[:, :], q[:, lo:hi], s[:, lo:hi], "vq " + k, ps, n)
-        if h: TC(T.yo[:, lo:hi], T[ps][:, 0:n], ps, "yo1", cost(n, 1))
-        else: AC(T.yo[:, lo:hi], T[ps][:, 0:n], ps, "yo0", plain(n))
-        dma("s", T.oc[:, 4 * lo:4 * hi], q[:, lo:hi].bitcast(dt.uint8), "d_out", k, "oc%d" % h, 100)
-        dma("s", T.y[:, lo:hi], T.yo[:, lo:hi], "d_out", "yo%d" % h, "y%d" % h, 100)
+        PC(T.yo[:, lo:hi], ps, n, "yo%d" % h, 1.0, "av"[::1 - 2 * h])
+    dma("s", T.oc[:, :], q[:, :].bitcast(dt.uint8), "d_out", xk, "oc", 160)
     for i in range(4):
-        dma("a", T.osc[4 * i:4 * i + 4, :], s[32 * i:32 * i + 4, :], "d_out", xk, "osc%d" % i)
+        dma("a" if i % 2 else "s", T.osc[4 * i:4 * i + 4, :], s[32 * i:32 * i + 4, :], "d_out", xk, "osc%d" % i)
+    for h, (lo, hi) in enumerate(PIECES):
+        dma("s", T.y[:, lo:hi], T.yo[:, lo:hi], "d_out", "yo%d" % h, "y%d" % h, 100)
 
-    if not ORDER: ORDER.extend(in_order(calls))
+    if not PLAN: PLAN.extend(planned(calls))
     count, token = {}, {}
     clock = {q: {} for q in Q}
 
@@ -336,9 +424,10 @@ def rank_program(g, core, T, topo):
             for k, v in list(snap.items()) + [(name, val)]:
                 clock[q][k] = max(clock[q].get(k, 0), v)
 
-    for i in ORDER:
+    for i, w in PLAN:
         c = calls[i]
-        q, sem = c["q"], c["sem"]
+        q, fn, t = c["ways"][w]
+        sem = c["sem"] or "c" + q
         count[sem] = count.get(sem, 0) + c["inc"]
         if q is None:
             token[i] = (sem, count[sem], {})
@@ -348,7 +437,7 @@ def rank_program(g, core, T, topo):
             t = token[d]
             if t[0] != "sent" and (t[0] not in best or best[t[0]][1] < t[1]): best[t[0]] = t
         for t in best.values(): need(q, *t)
-        done = c["fn"]()
+        done = fn()
         if sem != "sent": done.then_inc(T.sem[sem], c["inc"])
         token[i] = (sem, count[sem], dict(clock[q]))
     for name in SEMAPHORES:

from concourse.mybir import dt, AluOpType, ActivationFunctionType

N, C, MASK = 8, 320, [4, 1, 2]
BF, F4, I4, U2, CO, PL = "bfloat16", "float32", "int32", "uint16", "float8_e4m3fn_x4", "uint8"
POW = [1, 2, 4, 8, 16, 32, 64]
PIECES = [(0, 192), (192, C)]
HALVES = [(0, 160), (160, C)]
FIRST = [(0, 256), (256, C)]
HEAD = 337
ZB, ZT, XT = [0], [3], [3]
SCRATCH = {}


def _sb(dtype, **kw):
    for k, n in kw.items():
        SCRATCH[k] = ("sbuf", [128, n], dtype)


_sb(I4, nxi=20, jp=16, jpa=16)
_sb(BF, xin=4 * C, ut=512, vt=512, xt=4 * C, zt=4 * C, tb=4 * C, tp=4 * C, hb=4 * C, gb=4 * C, zb=4 * C,
    ones=516, ef=516, minus=2 * C, iotac=C, iotaT=C, dR=C, dX=C, dR16=16, rk=len(POW) * C, ws_=8 * C, wo=C,
    hr=C, gR=C, goR=C, posr=C, phr=C, ordr=C, w1=C, w2=C, lvc=C, svc=C, lcg=C, lvs=C, aR=C, bR=C,
    nv=2 * C, d1=2 * C, ff=HEAD + 2 * C, fb=16 + 2 * C + HEAD, cb=2 * C + 16)
_sb(F4, dI=16, mP=16, wn=16, wn2=1, c15=1, nc15=1, lv=20, sv=20, lw=20, l3=20, pos2=20, ph2=20, dq=20, kq=20, t0=20, t1=20, t2=20, nrr=C, yo=C)
_sb(U2, lk=20 * len(POW), k16=20, inv=20, ol=20, gl=20, hl=20, go=20, ql=20, pu=20, ul=8)
for _r in range(3):
    _sb(U2, **{"lab%d" % _r: 40, "rlab%d" % _r: 40})
    _sb(CO, **{"rq%d" % _r: C})
    _sb(PL, **{"rs%d" % _r: C})
    if _r: _sb(U2, **{"glab%d" % _r: 40})
for _r in range(4):
    _sb(CO, **{"xq%d" % _r: C})
    _sb(PL, **{"xs%d" % _r: C})
_sb(CO, zq=C, uq=128, uw=128, vq=128, wq=512, eq=512)
_sb(PL, zs=C, us=128, uws=128, vs=128, wsb=512, es=512)
for _r in range(8):
    SCRATCH["ps%d" % _r] = ("psum", [128, 512], F4)
SEMAPHORES = ["cv", "ct", "ca", "cg", "d_nx", "d_x", "d_u", "d_wc", "d_ws", "d_v", "d_out", "sent", "r_nx", "r_h"] + \
    ["r_%s%d" % (k, r) for k in "xl" for r in range(3)] + ["r_g%d" % r for r in (1, 2)]

PACES = [(0.83e-3, 1.3e-3, 3.2e-3, 0.15, 2.4), (1.15e-3, 2.1e-3, 5.5e-3, 0.12, 2.8)]
SLACK, REACH, PLAN, MEASURE = [0, 0] + [0.05 * 0.85 ** i for i in range(18)] + [0, 0], 8, [], []


def planned(calls):
    n = len(calls)
    queue, deps, hold = [[w[0] for w in c["ways"]] for c in calls], [c["deps"] for c in calls], [c["hold"] for c in calls]
    time = [[[w[2][0] + w[2][1] * p[0] + w[2][2] * p[1] + w[2][3] * p[2] for w in c["ways"]] for c in calls] for p in PACES]
    after, way = [[] for c in calls], [0] * n
    for i in range(n):
        for d in deps[i]: after[d].append(i)

    def run(order):
        total = 0.0
        for m in (1, 0):
            wait, tm, free, seen, start, rows = PACES[m][3], time[m], dict.fromkeys("vatgs", 0.0), [0.0] * n, [0.0] * n, 0.0
            for i in order:
                w = way[i]
                q = queue[i][w]
                t = free[q] if q else 0.0
                for d in deps[i]:
                    if seen[d] > t: t = seen[d]
                start[i] = t
                if q:
                    end = t + tm[i][w]
                    free[q] = t + hold[i] if hold[i] else end
                else:
                    end = rows = max(t + PACES[m][4], rows) + tm[i][w]
                seen[i] = end + wait
            total += (max(seen) + 0.03 * sum(start) / n) / (1 + m)
        return total, start

    order = list(range(n))
    measure, start = run(order)
    best = (measure, [(i, 0) for i in order])
    for slack in SLACK:
        for i in range(n):
            if queue[i][0] in (None, "s"): continue
            now, keep = order.index(i), way[i]
            rest = order[:now] + order[now + 1:]
            at = {k: p for p, k in enumerate(rest)}
            lo = max([0] + [at[d] + 1 for d in deps[i]])
            hi = min([n - 1] + [at[d] for d in after[i]])
            found = None
            for w, q in enumerate(queue[i]):
                marks = [p for p in range(lo, hi) if queue[rest[p]][way[rest[p]]] == q] + [hi]
                same = min(p for p in marks if p >= now) if w == keep else None
                marks.sort(key=lambda p: abs(p - now))
                for p in marks[:REACH]:
                    if p == same: continue
                    way[i] = w
                    trial = rest[:p] + [i] + rest[p:]
                    got, st = run(trial)
                    if got < measure + slack and (found is None or got < found[0]): found = (got, st, trial, w)
            way[i] = keep
            if found:
                measure, start, order, way[i] = found
                order.sort(key=lambda k: start[k])
                if measure < best[0]: best = (measure, [(k, way[k]) for k in order])
    MEASURE.append(best[0])
    return best[1]


def rank_program(g, core, T, topo):
    rank = T.rank_of(core)
    if rank is None:
        return
    A, ACT = AluOpType, ActivationFunctionType
    ve, te, sc, sy = g.vector, g.tensor, g.scalar, g.sync
    Q = {"v": ve, "t": te, "a": sc, "g": g, "s": sy}
    calls, wrote, read = [], {}, {}

    def op(ways, rd, wr, sem=None, inc=1, hold=None):
        rd, wr, i = rd.split(), wr.split(), len(calls)
        deps = [wrote[k] for k in rd]
        for k in wr: deps += read.get(k, []) + ([wrote[k]] if k in wrote else [])
        calls.append({"ways": ways, "deps": sorted(set(deps)), "hold": hold, "sem": sem, "inc": inc})
        for k in rd: read.setdefault(k, []).append(i)
        for k in wr: wrote[k], read[k] = i, []

    def dma(q, out, in_, sem, rd, wr, kb=0):
        op([(q, lambda: Q[q].dma_start(out, in_), (1.75 + kb / 200, 0, 0, 0))], rd, wr, sem, 16, 0.05)

    def send(dst, pieces, rsem, rd, wr, rows):
        rid, pid = topo.addr(dst, core)
        mask, n = topo.mask(core, dst), len(topo.engines(core, dst))

        def fn():
            for out, in_ in pieces: g.remote_dma(out, in_, T.sem[rsem], T.sem.sent, pid, rid, mask)
        op([("g", fn, (0.25 * len(pieces) + (rsem == "r_nx"), 0, 0, 0))], rd, "gone_" + rsem, "sent", n * len(pieces))
        op([(None, None, (rows, 0, 0, 0))], "gone_" + rsem, wr, rsem, n * len(pieces))

    def cyc(n=0, fixed=0.0): return (fixed, max(64, n), 0, 0)
    def picked(n, fixed=0.05): return (fixed, 0, n, 0)
    def strewn(n): return (0.05, 0, 0, n)
    def keys(name, lo, hi, step=1): return " ".join(name + str(i) for i in range(lo // step, (hi - 1) // step + 1))

    V = lambda fn, rd, wr, t: op([("v", fn, t)], rd, wr)
    TT = lambda out, a, b, o, rd, wr, t=cyc(): V(lambda: ve.tensor_tensor(out, a, b, o), rd, wr, t)
    TS = lambda out, a, s1, s2, o, o2, rd, wr, t=cyc(): V((lambda: ve.tensor_scalar(out, a, s1, s2, o, o2)) if o2 is not None else (lambda: ve.tensor_scalar(out, a, s1, None, o)), rd, wr, t)
    TC = lambda out, a, rd, wr, t=cyc(): V(lambda: ve.tensor_copy(out, a), rd, wr, t)
    SCAN = lambda out, a, b, i, o, o2, rd, wr, n: V(lambda: ve.tensor_tensor_scan(out, a, b, i, o, o2), rd, wr, cyc(n // 2))
    MS = lambda ap, c, wr, n=0: V(lambda: ve.memset(ap, c), "", wr, cyc(n // 2))
    QZ = lambda q, s, t, rd, wr, n: V(lambda: ve.quantize_mx(q, s, t), rd, wr, (0.012, n * 1.06, 0, 0))
    MM = lambda ps, l, ls, m, ms, rd, wr, n: op([("t", lambda: te.matmul_mx(ps, l, ls, m, ms, True, True), ((n + 16) * 0.9e-3, 0, 0, 0))], rd, wr)
    PLN = lambda buf, b, lo=0, hi=C: buf[:, C * b + lo:C * b + hi]

    def either(out, a, scale, bias, rd, wr, ta, tv, qs="av"):
        ways = {"a": (lambda: sc.activation(out, a, ACT.Identity if bias else ACT.Copy, bias=bias, scale=scale), ta),
                "v": (lambda: ve.tensor_scalar(out, a, scale, bias, A.mult, A.add) if bias else ve.tensor_scalar(out, a, scale, None, A.mult) if scale != 1.0 else ve.tensor_copy(out, a), tv)}
        op([(q,) + ways[q] for q in qs], rd, wr)

    GC = lambda out, a, rd, wr, n, scale=1.0, bias=0.0, qs="av": either(out, a, scale, bias, rd, wr, picked(n, 0.065), picked(n), qs)
    PC = lambda out, ps, n, wr, scale, qs="av": either(out, T[ps][:, 0:n], scale, 0.0, "", wr + " " + ps, cyc(n, 0.06), cyc(n), qs)
    S96, P96 = 2.0 ** -96, 2.0 ** 96
    partner = [T.cores[rank ^ m] for m in MASK]
    turn = [0]

    def weigh(src, rd):
        b = turn[0] = (turn[0] + 1) % 8
        SCAN(T.ws_[:, C * b:C * b + C], T.dR[:, :], src, 0.0, A.mult, A.add, rd + " dR", "ws_%d" % b, C)
        return T.ws_[:, C * b + 15:C * b + C:16], "ws_%d" % b

    def listed(out, wr, v, k): TS(out, v, T.wn[:, 15:16], 160.0, A.mult, A.add, k + " wn", wr)

    dma("s", T.nxi[:, :], T.nx[:, :], "d_nx", "", "nxi")
    dma("s", T.ut[:, :], T.u[:, :], "d_u", "", "ut", 131)
    dma("s", T.xin[:, :], T.x[:, :], "d_x", "", keys("xt0", 0, 4) + " " + keys("xt1", 0, 4), 460)
    dma("s", T.wq[:, :].bitcast(dt.uint8), T.wc[:, :], "d_wc", "", "wq", 720)
    dma("s", T.wsb[:, :], T.ws[:, :], "d_ws", "", "wsb", 790)
    dma("s", T.vt[:, :], T.v[:, :], "d_v", "", "vt", 920)

    MS(T.ones[:, :], 1.0, "ones", 516)
    op([("g", lambda: g.iota(T.jp[:, :], [[1, 16]], 0, -1), cyc(32, 0.13))], "", "jp")
    op([("g", lambda: g.affine_select(T.ef[:, :], T.ones[:, :], [[-1, 516]], A.is_equal, 0.0, 3, 4), cyc(1032, 0.17))], "ones", "ef")
    SCAN(T.iotac[:, :], T.ones[:, 0:C], T.ones[:, 0:C], -161.0, A.mult, A.add, "ones", "iotac", C)
    TS(T.iotaT[:, :], T.iotac[:, :], S96, None, A.mult, None, "iotac", "iotaT", cyc(C // 2))
    MS(T.iotaT[:, 160:161], S96 * 2.0 ** -20, "iotaT")
    TS(T.jpa[:, :], T.jp[:, :], 15, None, A.bitwise_and, None, "jp", "jpa")
    TS(T.dR16[:, :], T.jpa[:, :], 0.0, 16384.0, A.not_equal, A.mult, "jpa", "dR16")
    TS(T.nc15[:, :], T.jpa[:, 15:16], -1.0, None, A.mult, None, "jpa", "nc15")
    TS(T.k16[:, :], T.ones[:, 0:20], T.nc15[:, 0:1], 15.0, A.mult, A.add, "ones nc15", "k16")
    GC(T.dR[:, :], T.dR16[:, :].indirect(T.k16[:, :]), "dR16 k16", "dR", C)
    either(T.dX[:, :], T.dR[:, :], 257.0 / 16384.0, -256.0, "dR", "dX", cyc(C, 0.06), cyc(C // 2))
    TS(T.dI[:, :], T.dR16[:, :], 2.0 ** -28, None, A.mult, None, "dR16", "dI")
    TS(T.mP[:, :], T.jpa[:, :], 0.0, P96, A.is_equal, A.mult, "jpa", "mP")
    SCAN(T.wn[:, :], T.dI[:, :], T.mP[:, :], 0.0, A.mult, A.add, "dI mP", "wn", 0)
    TS(T.wn2[:, :], T.wn[:, 15:16], 2.0, None, A.mult, None, "wn", "wn2")
    TC(T.c15[:, :], T.jpa[:, 15:16], "jpa", "c15")
    MS(T.ordr[:, 0:16], -160.0 * S96, "or0")
    MS(T.ol[:, 0:1], 0, "ol0")
    TS(T.ul[:, :], T.iotac[:, 0:128:16], 160.0, None, A.add, None, "iotac", "ul")
    MS(T.minus[:, :], -1.0, "minus", 2 * C)
    MS(T.cb[:, 0:1], 160.0, "cb0")

    def xname(r): return T["xq%d" % r], T["xs%d" % r], "xq%d_0 xq%d_1" % (r, r)

    def quant(r, h):
        q, s, xk = xname(r)
        lo, hi = PIECES[h]
        QZ(q[:, lo:hi], s[:, lo:hi], (T.xt if r else T.xin)[:, 4 * lo:4 * hi], keys("xt%d" % h, 0, 4), "xq%d_%d" % (r, h), hi - lo)

    def scores(r, h):
        q, s, xk = xname(r)
        lo, hi = PIECES[h]
        n = hi - lo
        for i, w in ((1, T.w2), (0, T.w1)):
            ps = "ps%d" % (2 * h + i)
            MM(T[ps][:, 0:n], T.uw[:, :], T.uws[:, :], q[:, lo:hi], s[:, lo:hi], "uwc uws xq%d_%d" % (r, h), ps, n)
            ways = [("a", (lambda w=w, ps=ps: sc.activation(w[:, lo:hi], T[ps][:, 0:n], ACT.Sign, bias=-2.0 ** -100)), cyc(n, 0.06))]
            if i == 0: ways.insert(1 - (h and r > 0), ("v", (lambda ps=ps: ve.tensor_scalar(T.w1[:, lo:hi], T[ps][:, 0:n], 0.0, None, A.is_gt)), cyc(n)))
            op(ways, ps, "w%d%d" % (i + 1, h))

    def give_x(r):
        q, s, xk = xname(r)
        send(partner[r], [(T["rq%d" % r][:, :].bitcast(dt.uint8), q[:, :].bitcast(dt.uint8)), (T["rs%d" % r][:, :], s[:, :])], "r_x%d" % r, xk, "rq%d" % r, 2.8)

    def unpack(r, b, far, qs="av"):
        q, s, k = (T["rq%d" % r], T["rs%d" % r], "rq%d" % r) if far else xname(r)
        ps = "ps%d" % (b if far else 4 + b)
        MM(T[ps][:, 0:C], T.eq[:, 128 * b:128 * b + 128], T.es[:, 128 * b:128 * b + 128], q[:, :], s[:, :], "eq%d " % b + k, ps, C)
        PC(PLN(T.tp if far else T.tb, b), ps, C, ("tp" if far else "tb") + str(b), 0.5, qs)

    def runs(split):
        return [(lo, hi, [h]) for h, (lo, hi) in enumerate(PIECES)] if split else [(0, C, [0, 1])]

    def guests(r):
        if r == 0: return T.gl[:, :], T.hl[:, :], "gl", "hl"
        return T["glab%d" % r][:, 0:20], T["glab%d" % r][:, 20:40], "glab%d" % r, "glab%d" % r

    def places():
        v, k = weigh(T.posr[:, :], "posr")
        return v, k, lambda: TS(T.pos2[:, :], v, T.wn2[:, 0:1], 320.0, A.mult, A.add, k + " wn2", "pos2")

    def leavers(r):
        gL, hL, gk, hk = guests(r)
        TT(T.lvc[:, :], T.w1[:, :].indirect(hL), T.w2[:, :], A.is_lt, "w10 w11 w20 w21 " + hk, "lvc", picked(C))
        either(T.svc[:, :], T.lvc[:, :], -1.0, 1.0, "lvc", "svc", cyc(C, 0.06), cyc(C // 2))

    def flags_listed():
        SCAN(T.lvs[:, :], T.dX[:, :], T.lvc[:, :], 0.0, A.add, A.max, "dX lvc", "lvs", C)

    def quant_e(b):
        QZ(T.eq[:, 128 * b:128 * b + 128], T.es[:, 128 * b:128 * b + 128], T.ef[:, 3 - b:515 - b], "ef", "eq%d" % b, 128)

    def quant_u():
        QZ(T.uq[:, :], T.us[:, :], T.ut[:, :], "ut", "uq", 128)

    def pick_u():
        TC(T.uw[:, :].bitcast(dt.uint32), T.uq[:, :].bitcast(dt.uint32).indirect(T.ul[:, :]), "uq ul", "uwc", picked(128))
        op([("a", lambda: sc.activation(T.uws[:, :], T.us[:, :].indirect(T.ul[:, :]), ACT.Copy), picked(128, 0.065))], "uq ul", "uws")

    def place_of(i):
        TC(T.posr[:, :].indirect(T.ol[:, 4 * i:4 * i + 4]), T.iotaT[:, 64 * i:64 * i + 64], "iotaT ol%d" % i, "posr", strewn(64))

    def guest_cols(r):
        gL, hL, gk, hk = guests(r)
        GC(T.gR[:, :], T.iotaT[:, :].indirect(gL), "iotaT " + gk, "gR", C)

    def guest_leaves():
        TT(T.lcg[:, :], T.lvc[:, :].indirect(T.gl[:, :]), T.gR[:, :], A.mult, "lvc gR gl", "lcg", picked(C))

    def first_slots(i):
        lo, hi = FIRST[i]
        o, ok, n = T.ol[:, lo // 16:hi // 16], keys("ol", lo, hi, 64), hi - lo
        GC(T.d1[:, 2 * lo + 1:2 * hi:2], T.lcg[:, :].indirect(o), "lcg " + ok, "db%d" % i, n)
        GC(T.nv[:, 2 * lo:2 * hi:2], T.lvc[:, :].indirect(o), "lvc " + ok, "na%d" % i, n)
        TT(T.d1[:, 2 * lo:2 * hi:2], T.svc[:, :].indirect(o), T.ordr[:, lo:hi], A.mult, "svc %s %s" % (ok, keys("or", lo, hi, 64)), "da%d" % i, picked(n))
        TS(T.nv[:, 2 * lo + 1:2 * hi:2], T.d1[:, 2 * lo + 1:2 * hi:2], 0.0, None, A.is_equal, None, "db%d" % i, "nb%d" % i, cyc(n // 2))

    def by_flag():
        TS(T.lv[:, :], T.lvs[:, 15:C:16], T.c15[:, 0:1], None, A.subtract, None, "lvs c15", "lv")
        TS(T.sv[:, :], T.lv[:, :], -1.0, 1.0, A.mult, A.add, "lv", "sv")
        TS(T.lw[:, :], T.lv[:, :], T.wn2[:, 0:1], None, A.mult, None, "lv wn2", "lw")
        TS(T.l3[:, :], T.lv[:, :], 321.0, None, A.mult, None, "lv", "l3")

    RK = {m: T.rk[:, C * i:C * i + C] for i, m in enumerate(POW)}
    OL, OR = keys("ol", 0, C, 64), keys("or", 0, C, 64)
    quant_e(0)
    quant_e(1)
    TC(T.lk[:, 0:20], T.nxi[:, :], "nxi", "lk0")
    send(partner[0], [(T.gl[:, :], T.lk[:, 0:20])], "r_nx", "lk0", "gl", 0.55)
    TC(T.hr[:, :].indirect(T.lk[:, 0:20]), T.iotaT[:, :], "lk0 iotaT", "hr", strewn(C))
    listed(T.inv[:, :], "inv", *weigh(T.hr[:, :], "hr"))
    send(partner[0], [(T.hl[:, :], T.inv[:, :])], "r_h", "inv gone_r_nx", "hl", 0.55)
    beside = {2: [quant_u, lambda: quant(0, 1)], 4: [pick_u], 8: [lambda: quant(0, 0), lambda: scores(0, 0), lambda: scores(0, 1), lambda: give_x(0)],
              16: [lambda: quant_e(2), lambda: quant_e(3), lambda: guest_cols(0)], 32: [lambda: place_of(0)],
              64: [lambda: leavers(0), lambda: unpack(0, 0, False)], 128: [guest_leaves, lambda: unpack(0, 1, False)],
              192: [lambda: place_of(1), lambda: place_of(2), flags_listed, lambda: place_of(3), lambda: first_slots(0), by_flag], 256: [lambda: place_of(4)]}
    for i, m in enumerate(POW):
        win, wk, l = (T.iotaT[:, :], "iotaT", 0) if i == 0 else (RK[m // 2], keys("rk%d" % (i - 1), 0, 2), i - 1)
        if l: listed(T.lk[:, 20 * l:20 * l + 20], "lk%d" % l, *weigh(win, wk))
        for h, (lo, hi) in enumerate(HALVES if l else [(0, C)]):
            GC(T.rk[:, C * i + lo:C * i + hi], win.indirect(T.lk[:, 20 * l + lo // 16:20 * l + hi // 16]), wk + " lk%d" % l, "rk%d%d" % (i, h) if l else keys("rk%d" % i, 0, 2), hi - lo, qs="av"[::1 - 2 * h])
        for at in [m] if m < POW[-1] else range(m, C, m):
            n, lo, k = max(m, 16), at // 16 * 16, at // 64
            src = (at - m) // 16
            GC(T.ordr[:, at:at + n], RK[m].indirect(T.ol[:, src:src + n // 16]), keys("rk%d" % i, 0, 2) + " ol%d" % (src // 4), "or%d" % k, n)
            SCAN(T.wo[:, lo:lo + n], T.dR[:, 0:n], T.ordr[:, lo:lo + n], 0.0, A.mult, A.add, "dR or%d" % k, "wo%d" % k, n)
            listed(T.ol[:, lo // 16:(lo + n) // 16], "ol%d" % k, T.wo[:, lo + 15:lo + n:16], "wo%d" % k)
            for f in beside.get(at, []): f()

    DA, DB, NA, NB = (keys(k, 0, len(FIRST)) for k in ("da", "db", "na", "nb"))
    both = lambda k, b, hs: " ".join("%s%d%d" % (k, h, b) for h in hs)
    for r in range(3):
        lab, rlab, la, lb, rk = T["lab%d" % r], T["rlab%d" % r], "la%d" % r, "lb%d" % r, "rlab%d" % r
        last = r == 2
        if r == 0:
            first_slots(1)
            for h, (lo, hi) in enumerate(HALVES):
                GC(T.phr[:, lo:hi], T.posr[:, :].indirect(T.hl[:, lo // 16:hi // 16]), "posr hl", "phr%d" % h, hi - lo)
            places()[2]()
            v, k = weigh(T.phr[:, :], "phr0 phr1")
            TT(T.t0[:, :], T.pos2[:, :], T.sv[:, :], A.mult, "pos2 sv", "t0")
            TT(T.t1[:, :], v, T.lw[:, :], A.mult, k + " lw", "t1")
            TT(T.kq[:, :], T.t0[:, :], T.l3[:, :], A.add, "t0 l3", "kq")
        else:
            unpack(r, 0, False)
            leavers(r)
            TT(T.d1[:, 1:2 * C:2], T.lvc[:, :].indirect(T.go[:, :]), T.goR[:, :], A.mult, "lvc go goR", DB, picked(C))
            GC(T.nv[:, 0:2 * C:2], T.lvc[:, :].indirect(T.ol[:, :]), "lvc " + OL, NA, C)
            TT(T.d1[:, 0:2 * C:2], T.svc[:, :].indirect(T.ol[:, :]), T.ordr[:, :], A.mult, "svc " + OL + " " + OR, DA, picked(C))
            TS(T.nv[:, 1:2 * C:2], T.d1[:, 1:2 * C:2], 0.0, None, A.is_equal, None, DB, NB, cyc(C // 2))
            flags_listed()
            unpack(r, 1, False)
        unpack(r, 2, False)
        sl = " ".join([DA, DB, NA, NB])
        SCAN(T.ff[:, 0:HEAD], T.nv[:, 2 * C - HEAD:], T.d1[:, 2 * C - HEAD:], 0.0, A.mult, A.add, sl, "ff0", HEAD)
        if r: TT(T.t1[:, :], T.lvs[:, 15:C:16], T.dq[:, :], A.mult, "lvs dq", "t1")
        SCAN(T.fb[:, 15 + 2 * C + HEAD // 2:14 + 2 * C:-1], T.nv[:, HEAD - 1::-2], T.d1[:, HEAD - 1::-2], 0.0, A.mult, A.add, DA + " " + NA, "fb0", HEAD // 2 + 1)
        TT(T.t2[:, :], T.t1[:, :], T.kq[:, :], A.add, "t1 kq", "t2")
        SCAN(T.ff[:, HEAD:], T.nv[:, :], T.d1[:, :], T.ff[:, HEAD - 1:HEAD], A.mult, A.add, sl + " ff0", "ff1", 2 * C)
        TC(T.ql[:, :], T.t2[:, :], "t2", "ql")
        SCAN(T.fb[:, 14 + 2 * C:14:-1], T.nv[:, ::-1], T.d1[:, ::-1], T.fb[:, 15 + 2 * C:16 + 2 * C], A.mult, A.add, sl + " fb0", "fb1", 2 * C)
        GC(T.bR[:, :], T.ff[:, HEAD - 1:HEAD - 1 + 2 * C].indirect(T.ql[:, :]), "ff0 ff1 ql", "bR", C)
        for h, (lo, hi) in enumerate(PIECES):
            GC(T.aR[:, lo:hi], T.fb[:, 16:16 + 2 * C].indirect(T.ql[:, lo // 16:hi // 16]), "fb0 fb1 ql", "aR%d" % h, hi - lo, qs="va"[::1 - 2 * h])
        wb, wa = weigh(T.bR[:, :], "bR"), weigh(T.aR[:, :], "aR0 aR1")
        listed(lab[:, 20:40], lb, *wb)
        listed(lab[:, 0:20], la, *wa)
        send(partner[r], [(rlab[:, :], lab[:, :])], "r_l%d" % r, la + " " + lb, rk, 0.6)
        unpack(r, 3, False)

        def own_b(b, qs="av"): GC(PLN(T.gb, b), PLN(T.tb, b).indirect(lab[:, 20:40]), "tb%d " % b + lb, "gb%d" % b, C, qs=qs)
        if not last:
            n = r + 1
            send(partner[n], [(T["glab%d" % n][:, :], lab[:, :])], "r_g%d" % n, la + " " + lb + " gone_r_l%d" % r, "glab%d" % n, 0.6)
            SCAN(T.cb[:, 1:2 * C + 1], T.nv[:, :], T.minus[:, :], 160.0, A.add, A.add, NA + " " + NB + " minus", "cb", 2 * C)
            GC(T.posr[:, :], T.cb[:, 0:2 * C].indirect(T.ql[:, :]), "cb cb0 ql", "posr", C, -S96, qs="va")
            v, k, twice = places()
            listed(T.pu[:, :], "pu", v, k)
            twice()
            TC(T.ordr[:, :].indirect(T.pu[:, :]), T.iotaT[:, :], "pu iotaT", OR, strewn(C))
            listed(T.ol[:, :], OL, *weigh(T.ordr[:, :], OR))
            own_b(0); own_b(1)
            for b in range(4): unpack(r, b, True, "va" if b == 3 else "av")
            own_b(2); own_b(3)
        else:
            QZ(T.vq[:, :], T.vs[:, :], T.vt[:, :], "vt", "vq", 128)
            either(T.nrr[:, :], T.aR[:, :], P96, 160.0, "aR0 aR1", "nrr", cyc(C, 0.06), cyc(C))
            dma("s", T.nr[:, :], T.nrr[0:128:16, :], "d_out", "nrr", "nr")
            for b in range(4): own_b(b, "va")
            for b in range(4): unpack(r, b, True)
        for b in range(4):
            for lo, hi, hs in runs(b in ZB):
                GC(PLN(T.zb, b, lo, hi), PLN(T.tp, b).indirect(rlab[:, 20 + lo // 16:20 + hi // 16]), "tp%d " % b + rk, both("zb", b, hs), hi - lo, qs="va" if (b, hs) == (0, [0]) else "av")
        if not last:
            gL, hL, gk, hk = guests(r + 1)
            GC(T.phr[:, :], T.posr[:, :].indirect(hL), "posr " + hk, "phr0 phr1", C)
            guest_cols(r + 1)
        for h, (l0, h0) in enumerate(PIECES):
            for b in range(4):
                for lo, hi, hs in runs(b in ZT):
                    if hs[0] == h: TT(T.zt[:, 4 * lo + b:4 * hi:4], PLN(T.tp, b).indirect(rlab[:, lo // 16:hi // 16]), PLN(T.zb, b, lo, hi), A.add, "tp%d %s " % (b, both("zb", b, hs)) + rk, both("zt", b, hs), picked(hi - lo))
            QZ(T.zq[:, l0:h0], T.zs[:, l0:h0], T.zt[:, 4 * l0:4 * h0], keys("zt%d" % h, 0, 4), "zq%d" % h, h0 - l0)

        def layer(h, b, qs="av"):
            lo, hi = PIECES[h]
            n, ps = hi - lo, "ps%d" % (4 * h + b)
            MM(T[ps][:, 0:n], T.wq[:, 128 * b:128 * b + 128], T.wsb[:, 128 * b:128 * b + 128], T.zq[:, lo:hi], T.zs[:, lo:hi], "wq wsb zq%d" % h, ps, n)
            PC(PLN(T.hb, b, lo, hi), ps, n, "hb%d%d" % (h, b), 2.0 ** -6, qs)
        layer(0, 0); layer(0, 1)
        if not last:
            v, k = weigh(T.phr[:, :], "phr0 phr1")
            TS(T.ph2[:, :], v, T.wn2[:, 0:1], 321.0, A.mult, A.add, k + " wn2", "ph2")
        layer(1, 0, "va"); layer(1, 1)
        if not last:
            TT(T.dq[:, :], T.ph2[:, :], T.pos2[:, :], A.subtract, "ph2 pos2", "dq")
        for b in (2, 3): layer(0, b); layer(1, b)
        if not last:
            GC(T.goR[:, :], T.gR[:, :].indirect(T.ol[:, :]), "gR " + OL, "goR", C)
        for h in range(2):
            for b in range(4):
                for lo, hi, hs in runs(b in XT):
                    if hs[0] == h: TT(T.xt[:, 4 * lo + b:4 * hi:4], PLN(T.hb, b).indirect(lab[:, lo // 16:hi // 16]), PLN(T.gb, b, lo, hi), A.add, "hb0%d hb1%d gb%d " % (b, b, b) + la, both("xt", b, hs), picked(hi - lo))
            quant(r + 1, h)
            if not last:
                if h:
                    wg = weigh(T.goR[:, :], "goR")
                    TS(T.t0[:, :], T.dq[:, :], T.nc15[:, 0:1], None, A.mult, None, "dq nc15", "t0")
                    listed(T.go[:, :], "go", *wg)
                    TT(T.kq[:, :], T.t0[:, :], T.pos2[:, :], A.add, "t0 pos2", "kq")
                scores(r + 1, h)
        if not last: give_x(r + 1)

    q, s, xk = xname(3)
    for h, (lo, hi) in enumerate(PIECES):
        n, ps, k = hi - lo, "ps%d" % h, "xq3_%d" % h
        MM(T[ps][:, 0:n], T.vq[:, :], T.vs[:, :], q[:, lo:hi], s[:, lo:hi], "vq " + k, ps, n)
        PC(T.yo[:, lo:hi], ps, n, "yo%d" % h, 1.0, "av"[::1 - 2 * h])
    dma("s", T.oc[:, :], q[:, :].bitcast(dt.uint8), "d_out", xk, "oc", 160)
    for i in range(4):
        dma("a" if i % 2 else "s", T.osc[4 * i:4 * i + 4, :], s[32 * i:32 * i + 4, :], "d_out", xk, "osc%d" % i)
    for h, (lo, hi) in enumerate(PIECES):
        dma("s", T.y[:, lo:hi], T.yo[:, lo:hi], "d_out", "yo%d" % h, "y%d" % h, 100)

    if not PLAN: PLAN.extend(planned(calls))
    count, token = {}, {}
    clock = {q: {} for q in Q}

    def need(q, name, val, snap):
        if clock[q].get(name, 0) < val:
            Q[q].wait_ge(T.sem[name], val)
            for k, v in list(snap.items()) + [(name, val)]:
                clock[q][k] = max(clock[q].get(k, 0), v)

    for i, w in PLAN:
        c = calls[i]
        q, fn, t = c["ways"][w]
        sem = c["sem"] or "c" + q
        count[sem] = count.get(sem, 0) + c["inc"]
        if q is None:
            token[i] = (sem, count[sem], {})
            continue
        best = {}
        for d in c["deps"]:
            t = token[d]
            if t[0] != "sent" and (t[0] not in best or best[t[0]][1] < t[1]): best[t[0]] = t
        for t in best.values(): need(q, *t)
        done = fn()
        if sem != "sent": done.then_inc(T.sem[sem], c["inc"])
        token[i] = (sem, count[sem], dict(clock[q]))
    for name in SEMAPHORES:
        if count.get(name): need("s", name, count[name], {})
